import numpy as np, ml_dtypes
CORES = [25,29,65,69,153,157,193,197]
N = 8
import mx_ref
BF = ml_dtypes.bfloat16
def gentries(a):
    return np.ascontiguousarray(a.reshape(8, 16, -1).transpose(0, 2, 1)).reshape(8, -1)
def gtable(e):
    e = np.asarray(e); return np.ascontiguousarray(e.reshape(8, -1, 16).transpose(0, 2, 1)).reshape(128, -1).astype(np.int32)
def gcols(t, e):
    v = np.concatenate([t.reshape(8, 16, -1, 4), np.zeros((8, 16, 1, 4), BF)], axis=2)
    return np.ascontiguousarray(np.stack([v[g][:, e[g]] for g in range(8)])).reshape(128, -1)
def tile(rs):
    return np.stack(rs, axis=2).reshape(128, -1).astype(BF)
def cut(t, i, w=512):
    return t[:, w * i:w * i + w]
def pick(q, e):
    c = np.concatenate([q[0].reshape(128, -1, 4), np.zeros((128, 1, 4), np.uint8)], axis=1); s = np.concatenate([q[1], np.ones((16, 1), np.uint8)], axis=1)
    return (np.ascontiguousarray(c[:, e].reshape(128, -1)), np.ascontiguousarray(s[:, e]))
def join(*qs):
    return (np.concatenate([q[0] for q in qs], axis=1), np.concatenate([q[1] for q in qs], axis=1))
def put(q, e, v):
    c, s = q[0].reshape(128, -1, 4).copy(), q[1].copy(); c[:, e] = v[0].reshape(128, -1, 4); s[:, e] = v[1]
    return (c.reshape(128, -1), s)
def pk(c, s):
    return (np.ascontiguousarray(c), mx_ref.live(s))
def emit(q):
    return q[0], q[1]
def packed(v, rng):
    q = [mx_ref.quantize(np.ascontiguousarray(v[r])) for r in range(N)]
    return np.stack([a for a, b in q]), np.stack([mx_ref.plane(b, rng) for a, b in q])
def values_of_codes():
    e, c = np.zeros((128, 128, 4), np.float32), np.zeros((128, 2, 4), np.uint8)
    e[np.arange(128), np.arange(128), 0] = 1
    c[:127, :, 0] = np.arange(256).reshape(2, 128).T[:127]
    return mx_ref.matmul(mx_ref.quantize(e.reshape(128, 512).astype(BF)), (c.reshape(128, 8), np.full((16, 2), 127, np.uint8))).T.reshape(-1).astype(np.float64)
CODE_VALUE, SCALE_VALUE = values_of_codes(), 2.0 ** (np.arange(256) - 127.0)
def decode(q):
    return (CODE_VALUE[q[0]].reshape(16, 8, -1, 4) * SCALE_VALUE[q[1]][:, None, :, None] + 0.0).reshape(128, -1).astype(np.float32)
def f(rng, *shape):
    return mx_ref.flush((rng.standard_normal(shape, dtype=np.float32) * np.exp2(rng.integers(-2, 3, shape[:-1] + (1,)))).astype(BF))
def wide(rng, *shape, cols=0):
    v = rng.standard_normal(shape, dtype=np.float32) * np.exp2(rng.integers(-12, 13, shape)).astype(np.float32)
    if cols: v *= np.repeat(np.exp2(rng.integers(-cols, cols + 1, shape[:-2] + (1, shape[-1] // 4))) * (rng.random(shape[:-2] + (1, shape[-1] // 4)) > 0.0625), 4, axis=-1).astype(np.float32)
    return mx_ref.flush(v.astype(BF))
C, P, H, R = 288, 32, 40, 3
STEP = [1, 2, 4]
def play(s, n):
    place = np.arange(C)
    pile = np.repeat(np.arange(len(n)), n)
    o = np.lexsort((place, -s, pile))
    top = o[np.searchsorted(pile, np.arange(len(n)))]
    rest = np.delete(place, top)
    o = rest[np.lexsort((rest, s[rest], pile[rest]))]
    low = o[np.searchsorted(pile[rest], np.flatnonzero(n >= 2))]
    a, b = top[np.lexsort((top, -s[top]))], low[np.lexsort((low, s[low]))]
    left = np.delete(place, np.concatenate([top, low]))
    m = np.concatenate([np.maximum(n - 2, 0), [len(a), len(b)]])
    came = np.concatenate([left, C + np.arange(len(a)), C + H + np.arange(len(b))])
    k = np.repeat(np.arange(len(m)), m)
    e = came[np.lexsort((np.arange(C), k, -m[k]))]
    m = m[np.argsort(-m, kind="stable")]
    return a, b, e, m[m > 0]
def big(v):
    v = v.astype(np.float32)
    v[np.abs(v) < np.float32(2.0 ** -16)] = 0
    return v.astype(BF)
def sizes(rng, n, c, *shape):
    e = np.argsort(rng.random(shape + (c - 1,)), axis=-1)[..., :n - 1] + 1
    return np.diff(np.sort(e, axis=-1), axis=-1, prepend=0, append=c)
def pilelist(n):
    return np.stack([gtable(n[r]) for r in range(N)])
def numbers_of(rng):
    return {"x": big(f(rng, N, 128, 4 * C)), "u": np.array(f(rng, N, 128, 512)), "v": np.array(f(rng, N, 128, 512))}
def layers(rng):
    return big(f(rng, N, 128, 2048)).reshape(N, 8, 16, 4, 8, 16, 4)
def weights(rng, w):
    c, p = packed(np.ascontiguousarray(w).reshape(N, 128, 2048), rng)
    return {"wc": c, "ws": p}
def signs(rng):
    return np.stack([rng.permutation(8) % 2 * 2.0 - 1.0 for r in range(N)])
def setup_inputs(rng):
    return {**numbers_of(rng), **weights(rng, layers(rng)), "z": pilelist(sizes(rng, P, C, N, 8))}
def setup_inputs_ties(rng):
    d = numbers_of(rng)
    e = rng.permutation(N)
    x = d["x"].reshape(N, 8, 16, C, 4)
    for r in range(N):
        k = np.zeros(C, int) if r == e[0] else rng.permutation(C) % 3
        a = x[r][:, :8, :3].copy()
        a[:, :, 2] = 0
        x[r][:, :8] = a[:, :, k]
    x[e[1]] = 0
    u = d["u"].reshape(N, 8, 16, 128, 4)
    u[:, :, 8:, ::16] = 0
    w = layers(rng)
    w[:, :, 8:, :, :, :8] = 0
    return {"x": x.reshape(N, 128, 4 * C), "u": u.reshape(N, 128, 512), "v": d["v"], **weights(rng, w), "z": pilelist(sizes(rng, P, C, N, 8))}
def setup_inputs_near(rng):
    d = numbers_of(rng)
    x = np.zeros((N, 8, 16, C, 4), np.float32)
    u = d["u"].reshape(N, 128, 128, 4)
    u[:, :, ::16] = 0
    n = sizes(rng, P, C, N, 8)
    o, c = rng.permutation(N) % 4, signs(rng)
    upper = np.arange(C) // (C // 2)
    for r in range(N):
        i = (np.arange(C) + rng.integers(0, C, (8, 1))) % C
        if o[r] < 2:
            for g in np.flatnonzero(c[r] > 0)[:2]:
                last = int(np.sum(n[r, g, :int(np.argmax(n[r, g])) + 1])) - 1
                i[g] = (last - np.arange(C)) % C
        s = (i + 1) // 2
        size = 1.0 if o[r] < 2 else 2.0 ** -4
        if o[r] < 2: x[r, :, 0, :, 0] = c[r][:, None]
        if o[r] == 3:
            s = i % (C // 2)
            k = rng.permutation(8)
            for g in range(8):
                if k[g] % 2:
                    s[g] = (np.arange(C) - C // 4 - 1) % (C // 2)
                    n[r, g] = 1
                    n[r, g, rng.integers(P)] = C - P + 1
                else: n[r, g] = np.tile(sizes(rng, P // 2, C // 2), 2)
                more = upper ^ (k[g] // 2 % 2)
                x[r, g, 0, :, 0] = more * 4.5 * 2.0 ** -30
                x[r, g, 1, :, 0] = (1 - more) * 4.0 * 2.0 ** -30
        digit = ((s[:, :, None] >> np.arange(8)) & 1) * np.exp2(np.arange(8) - 23.0) * size
        x[r, :, 8] = digit[:, :, :4]
        x[r, :, 9] = digit[:, :, 4:]
        x[r, :, 10:] = rng.integers(4, 8, (8, 6, C, 4)) * 2.0 ** -20 * size
        q = 1.0 if o[r] == 0 else 2.0 ** -30
        for h in range(0, 128, 16):
            u[r, h, h, 0] = q
            u[r, h + 8:h + 10, h] = q
            if o[r] == 3:
                u[r, h, h, 0] = 1.125 * q
                u[r, h + 1, h, 0] = 1.25 * q
    w = layers(rng)
    w[:, :, :10] = 0
    w[:, :, :, :, :, :10] = 0
    return {"x": x.reshape(N, 128, 4 * C).astype(BF), "u": u.reshape(N, 128, 512), "v": d["v"], **weights(rng, w), "z": pilelist(n)}
def setup_inputs_huge(rng):
    d = numbers_of(rng)
    c = np.stack([rng.permutation(C) % 2 * 2.0 - 1.0 for r in range(N)])
    one = rng.permutation(N) < N // 2
    c[one] = -1
    x = (0.6 + 0.2 * rng.random((N, 128, C, 4))) * 2.0 ** 30
    u = d["u"].reshape(N, 128, 128, 4)
    a = 2.0 ** 30 * (1 - 0.25 * rng.random((N, 128, 8, 4)))
    for r in np.flatnonzero(one):
        for k in (x[r], a[r]):
            k[:] = 2.0 ** 30 * (1 - 0.0625 * rng.integers(0, 2, k.shape))
            k[::8, :, 0] = 2.0 ** 30
    x *= c[:, None, :, None]
    a *= signs(rng)[:, None, :, None]
    u[:, :, ::16] = a.astype(np.float32).astype(BF)
    w = np.zeros((N, 128, 4, 128, 4), np.float32)
    i = np.arange(128)
    for b in range(4): w[:, i, b, i, b] = 1
    return {"x": x.astype(np.float32).reshape(N, 128, 4 * C).astype(BF), "u": u.reshape(N, 128, 512), "v": d["v"], **weights(rng, w.astype(BF)), "z": pilelist(sizes(rng, P, C, N, 8))}
def oddsizes(rng, k):
    if k == 0: return 2 * R + sizes(rng, P, C - 2 * R * P)
    if k == 3: return rng.permutation(C // P + (np.arange(P) < C % P))
    if k == 4: return np.sort(sizes(rng, P, C))
    if k == 7: return np.sort(sizes(rng, P, C))[::-1]
    o = np.ones(P, int)
    if k == 8:
        i = np.sort(rng.permutation(P)[:2])
        o[i[0]] = (C - P + 2) // 2 - rng.integers(1, 9)
        o[i[1]] = C - P + 2 - o[i[0]]
        return o
    if k == 2: o += 1
    if k == 5: o += np.arange(P) % 2
    if k == 6: o += 2
    o[0] += C - np.sum(o)
    return rng.permutation(o)
def setup_inputs_ragged(rng):
    d = numbers_of(rng)
    h = int(rng.integers(8))
    n = np.stack([np.stack([oddsizes(rng, 8 if k == 1 and r % 2 else k) for k in np.insert(1 + rng.permutation(7), h, 0)]) for r in range(N)])
    x, u = d["x"].reshape(N, 128, C, 4), d["u"].reshape(N, 128, 128, 4)
    for r in range(0, N, 2):
        g = int(np.argmax(np.max(n[r], axis=1)))
        last = int(np.sum(n[r, g, :int(np.argmax(n[r, g])) + 1])) - 1
        k = big(u[r, :, 16 * g])
        x[r, :, last] = -k if r % 4 else k
    d["x"] = x.reshape(N, 128, 4 * C)
    return {**d, **weights(rng, layers(rng)), "z": pilelist(n)}
def setup_inputs_spread(rng):
    d = setup_inputs(rng)
    d["x"] = big(wide(rng, N, 128, 4 * C, cols=6))
    return d
def check_inputs(d):
    b = []
    for k in ("x", "u", "v"):
        a = np.abs(d[k].astype(np.float32))
        if not (np.isfinite(a).all() and ((a == 0) | (a >= 2.0 ** -30) & (a <= 2.0 ** 30)).all()): b.append("a value of " + k)
    none, least, most = [emit(mx_ref.quantize(np.full((128, 16), k, np.float32).astype(BF)))[1][0, 0] for k in (0.0, 2.0 ** -30, 2.0 ** 30)]
    for r in range(N):
        if ((d["wc"][r] == 0x7F) | (d["wc"][r] == 0xFF)).any(): b.append("wc: a code that is no number")
        s = mx_ref.live(d["ws"][r])
        if ((s != none) & ((s < least) | (s > most))).any(): b.append("ws: a scale out of range")
        n = gentries(d["z"][r]).astype(np.int64)
        if (n < 1).any(): b.append("z: a size under 1")
        if (np.sum(n, axis=1) != C).any(): b.append("z: a sum of sizes")
    return b
def reference(x, u, v, wc, ws, z):
    qu = [mx_ref.quantize(u[r]) for r in range(N)]
    lay = [pk(wc[r], ws[r]) for r in range(N)]
    now = [x[r] for r in range(N)]
    size = [list(gentries(z[r])) for r in range(N)]
    for t in range(R):
        given, sent, new = [], [], []
        for r in range(N):
            s = mx_ref.matmul(qu[r], mx_ref.quantize(now[r]))[::16] + np.float32(0.0)
            e, h = np.full((8, 2 * H), -1), np.zeros((8, C), int)
            for g in range(8):
                a, b, h[g], size[r][g] = play(s[g], size[r][g])
                e[g, :len(a)] = a
                e[g, H:H + len(b)] = b
            k = gcols(now[r], e)
            given.append(k)
            sent.append(mx_ref.quantize(k))
            new.append(h)
        came = decode(join(*sent))
        for r in range(N):
            k = given[r]
            d = cut(came, r ^ STEP[t], 8 * H)
            q = mx_ref.quantize(np.ascontiguousarray(((k.astype(np.float32) + d) * np.float32(0.5)).astype(BF)))
            c = tile([np.maximum(mx_ref.matmul(pick(lay[r], np.arange(128 * b, 128 * b + 128)), q), np.float32(0.0)) * np.float32(0.03125) + k[:, b::4].astype(np.float32) for b in range(4)])
            now[r] = gcols(np.concatenate([now[r], c], axis=1), new[r])
    y, oz = np.zeros((N, 128, C), np.float32), np.zeros((N, 8, H), np.float32)
    oc, osc = np.zeros((N, 128, 4 * C), np.uint8), np.zeros((N, 16, C), np.uint8)
    for r in range(N):
        q = mx_ref.quantize(now[r])
        y[r] = mx_ref.matmul(mx_ref.quantize(v[r]), q)
        for g in range(8): oz[r, g, :len(size[r][g])] = size[r][g]
        oc[r], osc[r] = emit(q)
    return {"y": y, "oz": oz, "oc": oc, "osc": osc}

@@ -1,0 +1,636 @@
+from concourse.bass import DstId, RemoteDMATransfer
+from concourse.mybir import dt, AluOpType, ActivationFunctionType
+
+C = 288
+ES = [32, 40, 40]
+STEP = [1, 2, 4]
+GC = C + 2
+XW = 4 * (GC + 80)
+PB = 296
+BIG = 2.0 ** 96
+KV = 32
+ONV = [(), ("ah", "dh"), ("ah", "lo")]
+CY, WAKE, LOOK, LEAD = 0.00104, 0.09, 0.03, 0.6
+HOP_LIST, HOP_X = [1.8, 3.8, 2.2], [2.8, 7.4, 3.8]
+
+f32, bf, i32, u16, u8, q4 = "float32", "bfloat16", "int32", "uint16", "uint8", "float8_e4m3fn_x4"
+SCRATCH = {}
+PER = {"nr": 48, "wi": 336, "rs": 2 * C, "st": 360, "me": 48, "eo": 6, "ei": 18, "cw": 72, "gs": 48, "pu": 4,
+       "ed": C, "eb": C, "ew": C, "sg": C, "sh": 48, "gl": 48, "t40": 40, "w80": 80}
+PART = {}
+
+
+def _sb(name, n, d):
+    SCRATCH[name] = ("sbuf", [128, n], d)
+
+
+def _parts(name, d, parts):
+    at = 0
+    for n, w in parts:
+        PART[n] = (name, at, w)
+        at += (w + 15) // 16 * 16
+    _sb(name, at, d)
+
+
+for _t in range(4):
+    _sb("xw%d" % _t, XW, bf)
+    _sb("qx%d" % _t, C, q4)
+    _sb("sx%d" % _t, C, u8)
+for _t in range(3):
+    _sb("ql%d" % _t, C, q4)
+    _sb("sl%d" % _t, C, u8)
+    _sb("of%d" % _t, 20, u16)
+    _sb("li%d" % _t, 20, u16)
+for _n, _k, _d in [("nr", 4, f32), ("wi", 4, bf), ("rs", 4, bf), ("st", 3, f32), ("me", 4, f32), ("eo", 3, u16), ("ei", 3, u16),
+                   ("cw", 3, f32), ("gs", 3, f32), ("pu", 4, u16), ("ed", 3, bf), ("eb", 3, bf), ("ew", 3, f32), ("sg", 3, f32),
+                   ("sh", 3, f32), ("gl", 3, f32), ("t40", 3, f32), ("w80", 3, f32)]:
+    _sb(_n, _k * PER[_n], _d)
+for _n, _w, _d in [
+    ("mq", C, q4), ("ms", C, u8), ("ml", 20, u16),
+    ("ut", 512, bf), ("vt", 512, bf), ("qu", 128, q4), ("su", 128, u8), ("qp", 128, q4), ("sp", 128, u8),
+    ("qv", 128, q4), ("sv", 128, u8), ("wq", 512, q4), ("wp", 512, u8), ("qe", 512, q4), ("se", 512, u8),
+    ("ft", 516, bf), ("ones", 592, bf), ("mt", 512, bf), ("qm", 128, q4), ("sm", 128, u8),
+    ("dh", 4 * GC, bf), ("ah", 320, bf), ("aa", 320, bf), ("rt", 320, f32), ("yt", C, f32),
+    ("pmm", 592, f32), ("nrec", 592, bf), ("dist", 592, bf), ("pi", 8, i32), ("zi", 8, i32), ("co", 52, u16), ("eo4", 72, u16),
+    ("ro", 6, u16), ("kr", 4, u16), ("inv", 4, u16),
+]:
+    _sb(_n, _w, _d)
+_parts("cf", f32, [("col", 16), ("jr", 72), ("jm", 80), ("tab", 64), ("md32", 64), ("md40", 80), ("kp32", 64), ("kp40", 80), ("qc", 72),
+                   ("kc", 48), ("dd", 144)])
+_parts("cb", bf, [("m16", 144), ("m16s", C), ("m4", C), ("ids", 48), ("nb", 32), ("w32", 260), ("w40", 486)])
+_parts("lf", f32, [("vm", 80), ("vw", 80), ("vr", 80), ("dg", 80), ("ix", 80), ("tt", 40), ("sr", 80), ("sw", 80), ("lh", 96), ("lg", 2 * C),
+                   ("lw", 2 * C), ("c1", 72), ("c2", 72), ("c3", 72), ("c4", 72)])
+_parts("lb", bf, [("sq32", 260), ("sq40", 486), ("rk", 486), ("kj", 144), ("kk", 96), ("sid", 48)])
+_parts("zf", f32, [("zb", 64), ("zt", 64), ("ve", 48), ("cn", 8), ("c0", 48), ("cu", 144), ("ky", 48), ("kw", 48), ("kx", 48), ("kb", 4),
+                   ("ka", 4), ("po", 48), ("p0", 32), ("pw", 144), ("zz", 144), ("px", 144)])
+for _t in range(6):
+    SCRATCH["ps%d" % _t] = ("psum", [128, 512], f32)
+
+SEMAPHORES = ["V", "S", "P", "G", "ldz", "ldx", "ldy", "ldu", "ldv", "ldw", "ldp", "sty", "stw", "stc", "std", "sts", "stz", "snd",
+              "qc0", "qc1", "qc2", "qs0", "qs1", "qs2", "ls0", "ls1", "ls2", "mc", "mp", "mi"]
+
+A = AluOpType
+F = ActivationFunctionType
+
+
+def nbits(m):
+    return bin(m).count("1")
+
+
+def relays_of(src, dst, T, topo):
+    return [c for c in topo.cores_of(src) if c != src and T.rank_of(c) is None and topo.die(c) == topo.die(src) and topo.may_write(c, dst)]
+
+
+def pieces(k):
+    return [(C * j // k, C * (j + 1) // k) for j in range(k)]
+
+
+def relay_program(g, core, T, topo):
+    for r, src in enumerate(T.cores):
+        for t in range(3):
+            dst = T.cores[r ^ STEP[t]]
+            if topo.may_write(src, dst):
+                continue
+            rl = relays_of(src, dst, T, topo)
+            if core not in rl:
+                continue
+            j = rl.index(core)
+            a, b = pieces(len(rl))[j]
+            got = len(topo.engines(src, core)) // len(rl)
+            rid, pid = topo.addr(dst, core)
+            m = topo.mask(core, dst)
+            sent = 0
+            g.wait_ge(T.sem.mc, got)
+            g.remote_dma(T["ql%d" % t][:, a:b].bitcast(dt.uint8), T.mq[:, a:b].bitcast(dt.uint8), T.sem["qc%d" % t], T.sem.snd, pid, rid, m)
+            g.wait_ge(T.sem.mp, got)
+            g.remote_dma(T["sl%d" % t][:, a:b], T.ms[:, a:b], T.sem["qs%d" % t], T.sem.snd, pid, rid, m)
+            sent += 2 * nbits(m)
+            if j == 0:
+                k = ES[t] // 2
+                g.wait_ge(T.sem.mi, len(topo.engines(src, core)))
+                g.remote_dma(T["li%d" % t][:, 0:k], T.ml[:, 0:k], T.sem["ls%d" % t], T.sem.snd, pid, rid, m)
+                sent += nbits(m)
+            g.wait_ge(T.sem.snd, sent)
+
+
+def clash(seen, outs, ins):
+    for regs, w in ((outs, True), (ins, False)):
+        for name, a, b in regs:
+            for lo, hi, wr, who in seen.get(name, []):
+                if lo < b and a < hi and (w or wr):
+                    yield who
+
+
+def enter(seen, outs, ins, who):
+    for regs, w in ((ins, False), (outs, True)):
+        for name, a, b in regs:
+            l = seen.setdefault(name, [])
+            if w:
+                l[:] = [e for e in l if not (a <= e[0] and e[1] <= b)]
+            l.append((a, b, w, who))
+
+
+def deal(calls):
+    seen, before, after = {}, [], [[] for c in calls]
+    for i, c in enumerate(calls):
+        before.append(set(clash(seen, c[1], c[2])))
+        enter(seen, c[1], c[2], i)
+        for j in before[i]:
+            after[j].append(i)
+    chain = [0.0] * len(calls)
+    for i in reversed(range(len(calls))):
+        chain[i] = calls[i][4] + calls[i][9] + max([WAKE + chain[j] for j in after[i]] + [0.0])
+    gate = [i for i, c in enumerate(calls) if c[1] and c[1][0][0] == "gl0"][0]
+    taken, begin = {}, [0.0] * len(calls)
+    for i in sorted(range(len(calls)), key=lambda i: -chain[i]):
+        at = max([begin[k] + calls[k][4] + WAKE for k in before[i]] + [0.0])
+        if calls[i][7] is True:
+            at = max(at, begin[gate] + calls[gate][3])
+        slots = taken.setdefault(calls[i][0], [])
+        k = 0
+        for k, (a, b) in enumerate(slots + [(1e9, 1e9)]):
+            if at + calls[i][3] <= a + LOOK:
+                break
+            at = max(at, b)
+        if calls[i][0]:
+            slots.insert(k, (at, at + calls[i][3]))
+        begin[i] = at
+    return [calls[i] for i in sorted(range(len(calls)), key=lambda i: (begin[i], -chain[i]))]
+
+
+def rank_program(g, core, T, topo):
+    rank = T.rank_of(core)
+    if rank is None:
+        relay_program(g, core, T, topo)
+        return
+    Q = {"V": g.vector, "S": g.scalar, "P": g.tensor, "G": g, "Y": g.sync}
+    calls = []
+
+    def R(name, a=0, b=None, s=1):
+        buf, at, w = PART.get(name, (name, 0, SCRATCH[name][1][1] if name in SCRATCH else 0))
+        b = w if b is None else b
+        ap = T[buf][:, at + a:at + b] if s == 1 else T[buf][:, at + a:at + b:s]
+        return (ap, [(name, a, b)], (b - a + s - 1) // s, 2 if SCRATCH[buf][2] == bf else 4)
+
+    def Rt(name, t, a=0, b=None, s=1):
+        return R(name, PER[name] * t + a, PER[name] * t + (PER[name] if b is None else b), s)
+
+    def As(x, name, a, b):
+        return (x[0], [(name, a, b)], x[2], x[3])
+
+    def I(win, off):
+        return (win[0].indirect(off[0]), win[1] + off[1], 16 * off[2], win[3], off[1])
+
+    def ap(x):
+        return x[0] if isinstance(x, tuple) else x
+
+    def add(q, outs, ins, busy, done, kind, f, sem=None, n=0):
+        o, i = [], [e for x in ins if isinstance(x, tuple) for e in x[1]]
+        for x in outs:
+            if isinstance(x, tuple):
+                i = i + (x[4] if len(x) == 5 else [])
+                o = o + (x[1][:1] if len(x) == 5 else x[1])
+        i = [(e[0], 0, 512) if e[0].startswith("ps") else e for e in i]
+        calls.append([q, o, i, busy, done, kind, f, sem, n, 0.0])
+
+    def run(q, outs, ins, f, cy=1.0, fix=0.0):
+        o, x = outs[0], ins[0] if ins else outs[0]
+        if len(o) == 5:
+            us = 0.05 + 3.8 * CY * o[2]
+        elif len(x) == 5:
+            us = 0.06 + 1.56 * CY * x[2]
+        elif fix:
+            us = fix + cy * CY * o[2]
+        else:
+            us = CY * max(64, cy * o[2])
+        add(q, outs, ins, us, us, "run", f)
+
+    def dma(q, sem, out, in_, us, n=16, also=()):
+        add(q, [out], [in_] + list(also), 0.05, us, "dma", lambda: Q[q].dma_start(ap(out), ap(in_)), sem, n)
+
+    v = g.vector
+
+    def fast(*xs):
+        return 0.5 if all(x[3] == 2 for x in xs) else 1.0
+
+    def cp(o, i):
+        run("V", [o], [i], lambda: v.tensor_copy(ap(o), ap(i)), fast(o, i))
+
+    def ms(o, c):
+        run("V", [o], [], lambda: v.memset(ap(o), c), fast(o))
+
+    def tt(o, a, b, op):
+        run("V", [o], [a, b], lambda: v.tensor_tensor(ap(o), ap(a), ap(b), op), 1.0 if b[1][0][0].startswith("ps") else 2.0)
+
+    def ts(o, a, s1, op0, s2=None, op1=None):
+        if op1 is None:
+            run("V", [o], [a, s1], lambda: v.tensor_scalar(ap(o), ap(a), ap(s1), None, op0), fast(o, a))
+        else:
+            run("V", [o], [a, s1, s2], lambda: v.tensor_scalar(ap(o), ap(a), ap(s1), ap(s2), op0, op1), fast(o, a))
+
+    def scan(o, d0, d1, init, op0, op1):
+        run("V", [o], [d0, d1, init], lambda: v.tensor_tensor_scan(ap(o), ap(d0), ap(d1), ap(init), op0, op1), fast(o, d0, d1))
+
+    def quant(qn, sn, a, b, src):
+        run("V", [R(qn, a, b), R(sn, a, b)], [src], lambda: v.quantize_mx(T[qn][:, a:b], T[sn][:, a:b], ap(src)), 1.06, 0.015)
+
+    def act(o, i, fn, bias=None, scale=None, accum=None):
+        kw = {}
+        if bias is not None:
+            kw["bias"] = ap(bias)
+        if scale is not None:
+            kw["scale"] = ap(scale)
+        if accum is not None:
+            kw["accum_out"] = ap(accum)
+        run("S", [o, accum], [i, bias, scale], lambda: g.scalar.activation(ap(o), ap(i), fn, **kw))
+
+    def mm(ps, lq, ls, la, rq, rs, a, b):
+        us = 1.2 * CY * (b - a + 16)
+        add("P", [R(ps)], [R(lq, la, la + 128), R(ls, la, la + 128), R(rq, a, b), R(rs, a, b)], us, us, "run",
+            lambda: g.tensor.matmul_mx(T[ps][:, 0:b - a], T[lq][:, la:la + 128], T[ls][:, la:la + 128], T[rq][:, a:b], T[rs][:, a:b], True, True))
+
+    def iota(o, pat, base, cm=0, small=True, late=False):
+        if small:
+            run("G", [o], [], lambda: g.iota(ap(o), pat, base, cm, allow_small_or_imprecise_dtypes=True), 2.0, 0.13)
+            calls[-1][7] = late
+        else:
+            run("G", [o], [], lambda: g.iota(ap(o), pat, base, cm), 2.0, 0.13)
+
+    def fill(o, c=0, late=False):
+        iota(o, [[0, o[2]]], c, late=late)
+
+    def wrap16(o, row):
+        scan(o, R("m16", 0, row[2]), row, 0.0, A.add, A.max)
+
+    def wrap4(o, row):
+        scan(o, R("m4", 0, row[2]), row, 0.0, A.add, A.max)
+
+    RC, R4, RM, P32, R1, R41, O16, C4, SA, SB, O16B, TMP, NR, R2 = [R("col", j, j + 1) for j in range(14)]
+
+    def J(a, n):
+        return R("jr", a, a + n)
+
+    def blocks(E):
+        if E == 32:
+            return [(0, 0, 15, 1.0), (1, 0, 31, 1.0), (2, 1, 47, -1.0), (3, 1, 63, -1.0)]
+        return [(0, 0, 15, 1.0), (1, 0, 31, 1.0), (2, 0, 39, SA), (2, 1, 47, SB), (3, 1, 63, -1.0), (4, 1, 79, -1.0)]
+
+    H = 4 * KV
+    dma("Y", "ldz", R("zi", 0, 2), T.z[:], 1.9)
+    dma("S", "ldu", R("ut"), T.u[:], 2.6)
+    dma("Y", "ldx", R("xw0", 0, 4 * H), T.x[:, 0:4 * H], 2.9)
+    dma("Y", "ldy", R("xw0", 4 * H, 4 * C), T.x[:, 4 * H:4 * C], 3.4)
+    x0 = [R("xw0", 0, 4 * C)]
+    dma("Y", "ldw", (T.wq[:].bitcast(dt.uint8),) + R("wq")[1:], T.wc[:], 3.5, also=x0)
+    dma("Y", "ldp", R("wp"), T.ws[:], 3.5, also=x0)
+    dma("Y", "ldv", R("vt"), T.v[:], 3.5, also=x0)
+
+    iota(R("pi", 0, 1), [[0, 1]], 0, 1, False)
+    iota(R("jr"), [[1, 72]], 0)
+    iota(R("jm"), [[0, 5], [1, 16]], 0)
+    ms(R("ones"), 1.0)
+    run("G", [R("ft")], [R("ones", 0, 516)], lambda: g.affine_select(T.ft[:], T.ones[:, 0:516], [[-1, 516]], A.is_equal, 0.0, 3, 4), 2.0, 0.17)
+    for b in range(4):
+        quant("qe", "se", 128 * b, 128 * b + 128, R("ft", 3 - b, 515 - b))
+    ms(R("c0"), 0.0)
+    ms(R("ve", 32, 48), 0.0)
+    fill(R("ve", 32, 33), ES[0] + 2)
+    fill(R("c0", 33, 34), C + ES[0])
+    fill(R("cu", 0, 144, 48))
+    for t in range(3):
+        fill(R("xw%d" % t, 4 * C, 4 * GC), late=t > 0)
+        fill(Rt("wi", t + 1), late=t > 0)
+    fill(R("dh", 4 * C, 4 * GC))
+    fill(R("lh", 32, 48))
+    fill(R("lh", 80, 96))
+    fill(R("mt", 256, 512), late=True)
+    fill(R("gs", 48, 144), late=True)
+    for t in (1, 2):
+        iota(Rt("gs", t, 32 + 2 * t, 34 + 2 * t), [[ES[t], 2]], C)
+    iota(R("dd"), [[0, 3], [1, 48]], C)
+    iota(R("qc"), [[4, 72]], -C)
+    ms(R("rs", 0, C), 0.0)
+    ms(R("nb"), -BIG)
+    fill(R("nrec", 0, 1))
+    fill(R("nrec", C + 1, PB + 1))
+    fill(R("nrec", PB + C + 1, 592))
+    fill(R("pmm", 0, 1))
+    ms(R("pmm", C + 1, PB + 1), -BIG)
+    ms(R("pmm", PB + C + 1, 592), BIG)
+    ts(R("pi", 1, 2), R("pi", 0, 1), 15, A.bitwise_and)
+    ts(R("pi", 2, 3), R("pi", 0, 1), 2, A.arith_shift_right, 3, A.bitwise_and)
+    ts(R("pi", 3, 4), R("pi", 0, 1), 3, A.bitwise_and)
+    ts(R("pi", 4, 5), R("pi", 0, 1), 31, A.bitwise_and)
+    cp(R("col", 0, 4), R("pi", 1, 5))
+    act(R("col", 4, 6), R("col", 0, 2), F.Identity, bias=1.0)
+    ts(R("co", 0, 2), J(0, 2), 32.0, A.mult, P32, A.add)
+    ts(R("co", 2, 10), J(0, 8), 16.0, A.mult)
+    ts(R("co", 10, 28), J(0, 18), 0.0, A.mult, RC, A.add)
+    ts(R("co", 28, 46), J(0, 18), 0.0, A.mult, RM, A.add)
+    ts(R("co", 46, 50), J(0, 4), 2.0, A.is_ge)
+    ts(R("tab", 0, 16), J(0, 16), RC, A.is_equal, -4096.0, A.mult)
+    ts(R("tab", 16, 32), J(0, 16), R1, A.is_equal, 1024.0, A.mult)
+    tt(R("tab", 32, 48), R("tab", 0, 16), R("tab", 16, 32), A.add)
+    ts(R("tab", 48, 52), J(0, 4), R4, A.is_equal, -4096.0, A.mult)
+    ts(R("tab", 52, 56), J(0, 4), R41, A.is_equal, 1024.0, A.mult)
+    tt(R("tab", 56, 60), R("tab", 48, 52), R("tab", 52, 56), A.add)
+    ts(O16, RC, 15.0, A.is_lt, 1024.0, A.mult)
+    ts(TMP, R4, 3.0, A.is_lt, -4096.0, A.mult)
+    ts(C4, TMP, 4.0 * C, A.add, RM, A.add)
+    ts(SA, RC, 8.0, A.is_lt)
+    act(SB, SA, F.Identity, bias=-1.0)
+    act(NR, RC, F.Copy, scale=-1.0)
+    act(R2, RC, F.Copy, scale=2.0)
+    act(O16B, O16, F.Identity, bias=1.0, scale=0.125)
+    act(R("ids"), J(0, 48), F.Identity, bias=1.0)
+    act(R("kc"), J(0, 48), F.Identity, bias=1.0, scale=-1.0 / 64)
+    act(R("qc"), R("qc"), F.Identity, bias=R4)
+    act(R("m16"), I(R("tab", 32, 48), R("co", 10, 19)), F.Copy)
+    act(R("m16s"), I(R("tab", 32, 48), R("co", 10, 28)), F.Copy, scale=0.125)
+    act(R("m4"), I(R("tab", 56, 60), R("co", 28, 46)), F.Copy)
+    for E in (32, 40):
+        L, w, sq, md = 2 * E + 1, "w%d" % E, "sq%d" % E, "md%d" % E
+        iota(R(w), [[E % 16, 2], [-16, len(blocks(E)) // 2], [1, L]], 0, late=E == 40)
+        act(R(w), R(w), F.Abs, bias=NR)
+        act(R(w), R(w), F.Sign, bias=-0.5)
+        act(R("kp%d" % E), R("jm", 0, 2 * E), F.Sign)
+        ts(R(md, 0, E), R("jm", 0, E), RC, A.is_equal, -1.0, A.mult)
+        ts(R(md, E, 2 * E), R("jm", E, 2 * E), RC, A.is_equal)
+        if E == 32:
+            act(R(sq, 2 * E, 4 * L, L), J(0, 4), F.Identity, bias=R2, scale=32.0)
+            fill(R(w, 0, 4 * L, L))
+        else:
+            act(R(sq, 2 * E, 2 * L, L), J(0, 2), F.Identity, bias=R2, scale=32.0)
+            act(R(sq, 4 * L - 1, 6 * L, L), J(2, 3), F.Identity, bias=R2, scale=32.0)
+            fill(R(sq, 3 * L - 1, 3 * L), late=True)
+            fill(R("kp40", E, E + 1), late=True)
+            fill(R(w, 0, 3 * L, L))
+            fill(R(w, 4 * L, 6 * L, L))
+
+    quant("qu", "su", 0, 128, R("ut"))
+    add("V", [R("qp")], [R("qu"), R("co", 2, 10)], 0.27, 0.27, "run",
+        lambda: v.tensor_copy(T.qp[:].bitcast(dt.uint32), T.qu[:].bitcast(dt.uint32).indirect(T.co[:, 2:10])))
+    add("S", [R("sp")], [R("su"), R("co", 2, 10)], 0.27, 0.27, "run",
+        lambda: g.scalar.activation(T.sp[:], T.su[:].indirect(T.co[:, 2:10]), F.Copy))
+    quant("qx0", "sx0", 0, H, R("xw0", 0, 4 * H))
+    quant("qx0", "sx0", H, C, R("xw0", 4 * H, 4 * C))
+    quant("qv", "sv", 0, 128, R("vt"))
+
+    cp(R("zb"), I(R("zi", 0, 2), R("co", 46, 50)))
+    run("V", [R("zt")], [R("zb")], lambda: v.transpose(ap(R("zt")), ap(R("zb"))))
+    cp(R("ve", 0, 32), I(R("zt"), R("co", 0, 2)))
+    scan(R("c0", 1, 33), R("ones", 0, 32), R("ve", 0, 32), 0.0, A.mult, A.add)
+    wrap16(R("p0"), R("c0", 0, 32))
+    ts(R("pu", 0, 2), R("p0", 15, 32, 16), O16, A.subtract)
+    cp(I(R("rs", 0, C), R("pu", 0, 2)), R("nb"))
+    act(R("rs", C, 2 * C), R("rs", 0, C), F.Copy, scale=-1.0)
+
+    def start(t, a=0, b=48):
+        return R("c0", a, b) if t == 0 else R("cu", 48 * (t - 1) + a, 48 * (t - 1) + b)
+
+    def ends(t):
+        E = ES[t]
+        n = R("ve", 0, E) if t == 0 else Rt("nr", t, 0, E)
+        act(Rt("st", t, 0, E), n, F.Relu, bias=-1.0)
+        act(Rt("st", t, 80 + E, 80 + 2 * E), Rt("st", t, 0, E), F.Sign, accum=R("cn", 1, 2) if t == 0 else None)
+        act(Rt("st", t, E, 2 * E), n, F.Relu, bias=-1.0)
+        e = Rt("st", t, 160, 160 + E) if t == 0 else Rt("t40", t, 0, E)
+        act(e, start(t, 1, 1 + E), F.Identity, bias=-(C + 1.0))
+        act(Rt("st", t, 320, 320 + E), start(t, 0, E), F.Identity, bias=1.0 - 2 * C, scale=2.0)
+        if t:
+            act(Rt("st", t, 80, 80 + E), n, F.Sign)
+            tt(Rt("st", t, 160, 160 + E), e, Rt("st", t, 80, 80 + E), A.mult)
+        tt(Rt("st", t, 160 + E, 160 + 2 * E), e, Rt("st", t, 80 + E, 80 + 2 * E), A.mult)
+        act(Rt("st", t, 240, 240 + E), Rt("st", t, 160, 160 + E), F.Identity, bias=C + 1.0)
+        act(Rt("st", t, 240 + E, 240 + 2 * E), Rt("st", t, 160 + E, 160 + 2 * E), F.Identity, bias=PB + C + 1.0)
+        wrap16(Rt("w80", t, 0, 2 * E), Rt("st", t, 240, 240 + 2 * E))
+        ts(Rt("eo", t, 0, E // 8), Rt("w80", t, 15, 2 * E, 16), O16, A.subtract)
+
+    ends(0)
+    act(R("ve", 33, 34), R("cn", 1, 2), F.Identity, bias=2.0)
+    for t in (1, 2, 3):
+        act(Rt("me", t), R("ve"), F.Relu, bias=-2.0 * t)
+        if t < 3:
+            act(Rt("me", 0), R("ve"), F.Relu, bias=-2.0 * t - 1)
+            act(R("kk", 0, 48), Rt("me", t), F.Sign, accum=R("cn", 2 * t, 2 * t + 1))
+            act(R("kk", 48, 96), Rt("me", 0), F.Sign, accum=R("cn", 2 * t + 1, 2 * t + 2))
+            act(R("ve", 32 + 2 * t, 34 + 2 * t), R("cn", 2 * t, 2 * t + 2), F.Identity, bias=2.0 * t + 2)
+    tt(R("ky"), R("ve"), R("kc"), A.add)
+    wrap16(R("kw"), R("ky"))
+    ts(R("kb", 0, 3), R("kw", 15, 48, 16), -1.0, A.mult, O16, A.add)
+    for k in range(3):
+        act(R("kj", 48 * k, 48 * k + 48), R("ky"), F.Sign, bias=R("kb", k, k + 1), accum=R("ka", k, k + 1))
+    ts(R("kr", 0, 3), R("ka", 0, 3), 0.5, A.mult, 23.5, A.add)
+    cp(I(R("sid"), R("kr", 0, 3)), R("ids"))
+    wrap16(R("kx"), R("sid"))
+    ts(R("inv", 0, 3), R("kx", 15, 48, 16), O16, A.subtract, -1.0, A.add)
+    for t in (1, 2, 3):
+        k = 48 * (t - 1)
+        act(Rt("nr", t), I(Rt("me", t), R("inv", 0, 3)), F.Copy)
+        scan(R("cu", k + 1, k + 48), R("ones", 0, 47), Rt("nr", t, 0, 47), 0.0, A.mult, A.add)
+        act(R("zz", k, k + 48), Rt("nr", t), F.Copy, scale=-1000.0)
+        tt(R("zz", k, k + 48), R("zz", k, k + 48), R("dd", k, k + 48), A.add)
+        tt(R("px", k, k + 48), R("zz", k, k + 48), start(t), A.max)
+        wrap16(R("pw", k, k + 48), R("px", k, k + 48))
+        ts(Rt("pu", t, 0, 3), R("pw", k + 15, k + 48, 16), O16, A.subtract)
+        cp(I(Rt("wi", t), Rt("pu", t, 0, 3)), R("sid") if t == 1 else R("ids"))
+        act(Rt("rs", t, 0, C), Rt("wi", t, 0, C), F.Copy, scale=-BIG / 64)
+        if t < 3:
+            act(Rt("rs", t, C, 2 * C), Rt("wi", t, 0, C), F.Copy, scale=BIG / 64)
+            ends(t)
+    dma("Y", "stz", T.oz[:], (T.nr[0:128:16, 3 * 48:3 * 48 + 40],) + Rt("nr", 3)[1:], 2.0)
+    act(R("po"), I(start(1), R("kr", 0, 3)), F.Copy)
+    for t in range(3):
+        if t == 0:
+            tt(Rt("sh", 0), start(0), R("po"), A.subtract)
+        else:
+            act(Rt("gl", t), I(Rt("gs", t), R("inv", 0, 3)), F.Copy)
+            tt(Rt("gl", t), Rt("gl", t), start(t), A.max)
+            tt(Rt("sh", t), Rt("gl", t), start(t + 1), A.subtract)
+        scan(Rt("ed", t), Rt("rs", t + 1, 0, C), Rt("wi", t + 1, 0, C), 0.0, A.add, A.max)
+        scan(Rt("eb", t), R("m16s"), Rt("ed", t), 0.0, A.add, A.max)
+        ts(Rt("ei", t), Rt("eb", t, 15, C, 16), O16B, A.subtract)
+        act(Rt("sg", t), I(Rt("sh", t), Rt("ei", t)), F.Copy)
+        wrap4(Rt("ew", t), Rt("sg", t))
+        tt(Rt("cw", t), Rt("ew", t, 3, C, 4), R("qc"), A.add)
+
+    sent = [0]
+
+    def send_x(t):
+        dst = T.cores[rank ^ STEP[t]]
+        qx, sx = "qx%d" % t, "sx%d" % t
+        if topo.may_write(core, dst):
+            rid, pid = topo.addr(dst, core)
+            m = topo.mask(core, dst)
+
+            def f():
+                g.remote_dma(T["ql%d" % t][:].bitcast(dt.uint8), T[qx][:].bitcast(dt.uint8), T.sem["qc%d" % t], T.sem.snd, pid, rid, m)
+                g.remote_dma(T["sl%d" % t][:], T[sx][:], T.sem["qs%d" % t], T.sem.snd, pid, rid, m)
+            sent[0] += 2 * nbits(m)
+            got = nbits(topo.mask(dst, core))
+        else:
+            rl = relays_of(core, dst, T, topo)
+            both = []
+            for codes in (True, False):
+                tr = []
+                for j, c in enumerate(rl):
+                    a, b = pieces(len(rl))[j]
+                    en = topo.engines(core, c)
+                    k = len(en) // len(rl)
+                    m = sum(1 << e for e in en[j * k:j * k + k])
+                    rid, pid = topo.addr(c, core)
+                    if codes:
+                        tr.append(RemoteDMATransfer(dst_ids=[DstId(rid=rid, pnc=pid)], dma_engine_mask=m, remote_sem=T.sem.mc,
+                                                    src=T[qx][:, a:b].bitcast(dt.uint8), dst=T.mq[:, a:b].bitcast(dt.uint8)))
+                    else:
+                        tr.append(RemoteDMATransfer(dst_ids=[DstId(rid=rid, pnc=pid)], dma_engine_mask=m, remote_sem=T.sem.mp,
+                                                    src=T[sx][:, a:b], dst=T.ms[:, a:b]))
+                    sent[0] += k
+                both.append(tr)
+
+            def f():
+                for tr in both:
+                    g.remote_dma_fused(tr, local_sem=T.sem.snd)
+            got = sum(nbits(topo.mask(c, core)) for c in relays_of(dst, core, T, topo))
+        gone = (None, [("gx%d" % t, 0, 1)])
+        add("G", [gone], [R(qx), R(sx)], 0.6, HOP_X[t], "send", f)
+        add(None, [R("ql%d" % t)], [gone], 0.0, 0.0, "land", None, "qc%d" % t, got)
+        add(None, [R("sl%d" % t)], [gone], 0.0, 0.0, "land", None, "qs%d" % t, got)
+
+    def send_list(t):
+        dst = T.cores[rank ^ STEP[t]]
+        k = ES[t] // 2
+        if topo.may_write(core, dst):
+            to, land, sem, frm = dst, "li%d" % t, "ls%d" % t, dst
+        else:
+            to, land, sem, frm = relays_of(core, dst, T, topo)[0], "ml", "mi", relays_of(dst, core, T, topo)[0]
+        rid, pid = topo.addr(to, core)
+        m = topo.mask(core, to)
+        sent[0] += nbits(m)
+        gone = (None, [("gl%d" % t, 0, 1)])
+        add("G", [gone], [R("of%d" % t, 0, k)], 0.3, HOP_LIST[t], "send",
+            lambda: g.remote_dma(T[land][:, 0:k], T["of%d" % t][:, 0:k], T.sem[sem], T.sem.snd, pid, rid, m))
+        add(None, [R("li%d" % t, 0, k)], [gone], 0.0, 0.0, "land", None, "ls%d" % t, nbits(topo.mask(frm, core)))
+
+    for t in range(3):
+        E, xw = ES[t], "xw%d" % t
+        L, bl, sq, K = 2 * E + 1, blocks(E), "sq%d" % E, E // 8
+        eo, of, cw = Rt("eo", t, 0, K), R("of%d" % t, 0, E // 2), Rt("cw", t)
+        mm("ps0", "qp", "sp", 0, "qx%d" % t, "sx%d" % t, 0, H)
+        mm("ps5", "qp", "sp", 0, "qx%d" % t, "sx%d" % t, H, C)
+        send_x(t)
+        two = [(0, H, R("ps0", 0, H)), (H, C, R("ps5", 0, C - H))]
+        for a, b, s in two:
+            scan(R("pmm", 1 + a, 1 + b), Rt("rs", t, a, b), s, R("pmm", a, a + 1) if a else 0.0, A.add, A.max)
+            scan(R("pmm", PB + 1 + a, PB + 1 + b), Rt("rs", t, C + a, C + b), s, R("pmm", PB + a, PB + a + 1) if a else 0.0, A.add, A.min)
+        tt(R("vm", 0, 2 * E), I(R("pmm"), eo), R("md%d" % E), A.mult)
+        act(R("vr", 0, 2 * E), I(R("pmm"), eo), F.Copy)
+        scan(R("vw", 0, 2 * E), R("kp%d" % E), R("vm", 0, 2 * E), 0.0, A.mult, A.add)
+        calls[-1][9] = LEAD
+        for j, (k, l, bc, sc) in enumerate(bl):
+            act(R(sq, j * L + E, j * L + 2 * E), R("vr", l * E, l * E + E), F.Sign, bias=R("vw", bc, bc + 1), scale=sc)
+        for j in range(len(bl)):
+            act(R(sq, j * L, j * L + E), R(sq, j * L + E, j * L + 2 * E), F.Square)
+        for a, b, s in two:
+            tt(R("nrec", 1 + a, 1 + b), R("pmm", a, b), s, A.is_ge)
+            tt(R("nrec", PB + 1 + a, PB + 1 + b), R("pmm", PB + a, PB + b), s, A.is_le)
+        scan(R("dist"), R("ones"), R("nrec"), 0.0, A.add, A.mult)
+        tt(R("dg", 0, 2 * E), I(R("dist"), eo), Rt("st", t, 0, 2 * E), A.min)
+        tt(R("ix", 0, 2 * E), Rt("st", t, 160, 160 + 2 * E), R("dg", 0, 2 * E), A.subtract)
+        tt(R("tt", 0, E), Rt("st", t, 320, 320 + E), R("ix", 0, E), A.subtract)
+        tt(R("ix", E, 2 * E), R("ix", E, 2 * E), R("tt", 0, E), A.max)
+        scan(R("rk", 0, L * len(bl)), R("w%d" % E), R(sq), 0.0, A.mult, A.add)
+        if E == 32:
+            ts(R("ro", 0, 4), R("rk", L - 1, 4 * L, L), 0.5, A.mult)
+        else:
+            ts(R("ro", 0, 2), R("rk", L - 1, 2 * L, L), 0.5, A.mult)
+            ts(R("ro", 2, 5), R("rk", 4 * L - 1, 6 * L, L), 0.5, A.mult)
+        cp(I(R("sr", 0, 2 * E), R("ro", 0, K)), R("ix", 0, 2 * E))
+        wrap4(R("sw", 0, 2 * E), R("sr", 0, 2 * E))
+        ts(of, R("sw", 3, 2 * E, 4), 4.0, A.mult, C4, A.add)
+        send_list(t)
+        if "ah" in ONV[t]:
+            ts(R("ah", 0, 8 * E), I(R(xw, 0, 4 * GC), of), 0.5, A.mult)
+        else:
+            act(R("ah", 0, 8 * E), I(R(xw, 0, 4 * GC), of), F.Copy, scale=0.5)
+        act(R("aa", 0, 8 * E), R("ah", 0, 8 * E), F.Copy, scale=2.0)
+        tt(R("lh", 0, E), R("ix", 0, E), R("ix", E, 2 * E), A.min)
+        tt(R("lh", 48, 48 + E), R("ix", 0, E), R("ix", E, 2 * E), A.max)
+        if "lo" in ONV[t]:
+            cp(R("lg", 0, C), I(R("lh", 0, 48), Rt("ei", t)))
+        else:
+            act(R("lg", 0, C), I(R("lh", 0, 48), Rt("ei", t)), F.Copy)
+        act(R("lg", C, 2 * C), I(R("lh", 48, 96), Rt("ei", t)), F.Identity, bias=-1.0)
+        wrap4(R("lw", 0, C), R("lg", 0, C))
+        wrap4(R("lw", C, 2 * C), R("lg", C, 2 * C))
+        tt(R("c1"), R("lw", 3, C, 4), cw, A.is_le)
+        tt(R("c2"), R("lw", C + 3, 2 * C, 4), cw, A.is_le)
+        tt(R("c3"), R("c1"), cw, A.add)
+        tt(R("c4"), R("c3"), R("c2"), A.add)
+        ts(R("eo4"), R("c4"), 4.0, A.mult, C4, A.add)
+        for b in range(4):
+            mm("ps%d" % (1 + b), "qe", "se", 128 * b, "ql%d" % t, "sl%d" % t, 0, C)
+            o = As(R("dh", b, 4 * C, 4), "dh", C * b, C * b + C)
+            if "dh" in ONV[t] and b % 2:
+                ts(o, R("ps%d" % (1 + b), 0, C), 0.5, A.mult)
+            else:
+                act(o, R("ps%d" % (1 + b), 0, C), F.Copy, scale=0.5)
+        tt(R("mt", 0, 8 * E), I(R("dh"), R("li%d" % t, 0, E // 2)), R("ah", 0, 8 * E), A.add)
+        quant("qm", "sm", 0, 128, R("mt"))
+        for b in range(4):
+            mm("ps%d" % (1 + b), "wq", "wp", 128 * b, "qm", "sm", 0, 128)
+            act(R("rt", 80 * b, 80 * b + 2 * E), R("ps%d" % (1 + b), 0, 2 * E), F.Relu, scale=0.03125)
+            tt(As(R(xw, 4 * GC + b, 4 * GC + 8 * E, 4), xw, 4 * GC + 80 * b, 4 * GC + 80 * b + 80),
+               R("rt", 80 * b, 80 * b + 2 * E), R("aa", b, 8 * E, 4), A.add)
+        xn, win = "xw%d" % (t + 1), As(R(xw, 0, 4 * GC + 8 * E), xw, 0, XW)
+        act(R(xn, 4 * H, 4 * C), I(win, R("eo4", KV, 72)), F.Copy)
+        cp(R(xn, 0, 4 * H), I(win, R("eo4", 0, KV)))
+        quant("qx%d" % (t + 1), "sx%d" % (t + 1), 0, H, R(xn, 0, 4 * H))
+        quant("qx%d" % (t + 1), "sx%d" % (t + 1), H, C, R(xn, 4 * H, 4 * C))
+
+    mm("ps0", "qv", "sv", 0, "qx3", "sx3", 0, H)
+    mm("ps1", "qv", "sv", 0, "qx3", "sx3", H, C)
+    act(R("yt", 0, H), R("ps0", 0, H), F.Copy)
+    cp(R("yt", H, C), R("ps1", 0, C - H))
+    dma("Y", "stc", T.oc[:, 0:4 * H], (T.qx3[:, 0:H].bitcast(dt.uint8),) + R("qx3", 0, H)[1:], 2.3)
+    dma("Y", "std", T.oc[:, 4 * H:4 * C], (T.qx3[:, H:C].bitcast(dt.uint8),) + R("qx3", H, C)[1:], 2.3)
+    dma("S", "stw", T.y[:, 0:H], R("yt", 0, H), 2.3)
+    dma("Y", "sty", T.y[:, H:C], R("yt", H, C), 2.3)
+    for k in range(4):
+        dma("S", "sts", T.osc[4 * k:4 * k + 4, :], (T.sx3[32 * k:32 * k + 4, :],) + R("sx3")[1:], 2.0, 64)
+
+    cnt = {"V": 0, "S": 0, "P": 0, "G": 0}
+    known = {q: {} for q in Q}
+    clock, seen, owed = {}, {}, {}
+
+    def need(q, sem, n):
+        if known[q].get(sem, 0) >= n:
+            return
+        Q[q].wait_ge(T.sem[sem], n)
+        known[q][sem] = n
+        for s, k in clock.get((sem, n), {}).items():
+            known[q][s] = max(known[q].get(s, 0), k)
+
+    for q, outs, ins, busy, done, kind, f, sem, n, lead in deal(calls):
+        if kind == "land":
+            owed[sem] = n
+            enter(seen, outs, [], (sem, n))
+            continue
+        want = {}
+        for s, k in clash(seen, outs, ins):
+            want[s] = max(want.get(s, 0), k)
+        for s in sorted(want, key=lambda s: s == q):
+            need(q, s, want[s])
+        if kind == "send":
+            f()
+            continue
+        if kind == "run":
+            cnt[q] += 1
+            sem, n = q, cnt[q]
+        f().then_inc(T.sem[sem], 16 if kind == "dma" else 1)
+        clock[(sem, n)] = dict(known[q])
+        owed[sem] = n
+        enter(seen, outs, ins, (sem, n))
+    g.wait_ge(T.sem.snd, sent[0])
+    for s, n in owed.items():
+        need("Y", s, n)

@@ -1,4 +1,3 @@
-from concourse.bass import DstId, RemoteDMATransfer
 from concourse.mybir import dt, AluOpType, ActivationFunctionType
 
 C = 288
@@ -9,9 +8,10 @@ XW = 4 * (GC + 80)
 PB = 296
 BIG = 2.0 ** 96
 KV = 32
-ONV = [(), ("ah", "dh"), ("ah", "lo")]
-CY, WAKE, LOOK, LEAD = 0.00104, 0.09, 0.03, 0.6
-HOP_LIST, HOP_X = [1.8, 3.8, 2.2], [2.8, 7.4, 3.8]
+SPLIT = [False, True, False]
+ONV = [("rs", "sg"), ("ah", "dh", "rs"), ("ah", "lo", "rs")]
+CY, WAKE, LEAD, EARLY, FIRST = 0.00104, 0.14, 0.6, 1.0, 1.8
+HOP_LIST, HOP_X = [2.2, 4.6, 2.6], [3.2, 7.0, 4.4]
 
 f32, bf, i32, u16, u8, q4 = "float32", "bfloat16", "int32", "uint16", "uint8", "float8_e4m3fn_x4"
 SCRATCH = {}
@@ -67,7 +67,8 @@ for _t in range(6):
     SCRATCH["ps%d" % _t] = ("psum", [128, 512], f32)
 
 SEMAPHORES = ["V", "S", "P", "G", "ldz", "ldx", "ldy", "ldu", "ldv", "ldw", "ldp", "sty", "stw", "stc", "std", "sts", "stz", "snd",
-              "qc0", "qc1", "qc2", "qs0", "qs1", "qs2", "ls0", "ls1", "ls2", "mc", "mp", "mi"]
+              "qc0", "qc1", "qc2", "qs0", "qs1", "qs2", "ls0", "ls1", "ls2", "qd0", "qd1", "qd2", "qt0", "qt1", "qt2",
+              "mc", "mp", "md", "mr", "mi"]
 
 A = AluOpType
 F = ActivationFunctionType
@@ -81,8 +82,9 @@ def relays_of(src, dst, T, topo):
     return [c for c in topo.cores_of(src) if c != src and T.rank_of(c) is None and topo.die(c) == topo.die(src) and topo.may_write(c, dst)]
 
 
-def pieces(k):
-    return [(C * j // k, C * (j + 1) // k) for j in range(k)]
+def pieces(t):
+    p = [(0, 4 * KV), (4 * KV, C)] if SPLIT[t] else [(0, C)]
+    return [(a, b, "q%s%d" % ("cd"[j], t), "q%s%d" % ("st"[j], t), "m" + "cd"[j], "m" + "pr"[j]) for j, (a, b) in enumerate(p)]
 
 
 def relay_program(g, core, T, topo):
@@ -94,23 +96,24 @@ def relay_program(g, core, T, topo):
             rl = relays_of(src, dst, T, topo)
             if core not in rl:
                 continue
-            j = rl.index(core)
-            a, b = pieces(len(rl))[j]
-            got = len(topo.engines(src, core)) // len(rl)
+            got = nbits(topo.mask(src, core))
             rid, pid = topo.addr(dst, core)
             m = topo.mask(core, dst)
             sent = 0
-            g.wait_ge(T.sem.mc, got)
-            g.remote_dma(T["ql%d" % t][:, a:b].bitcast(dt.uint8), T.mq[:, a:b].bitcast(dt.uint8), T.sem["qc%d" % t], T.sem.snd, pid, rid, m)
-            g.wait_ge(T.sem.mp, got)
-            g.remote_dma(T["sl%d" % t][:, a:b], T.ms[:, a:b], T.sem["qs%d" % t], T.sem.snd, pid, rid, m)
-            sent += 2 * nbits(m)
-            if j == 0:
+            for j, (a, b, sc, ss, rc, rs) in enumerate(pieces(t)):
+                if rl[j % len(rl)] == core:
+                    g.wait_ge(T.sem[rc], got)
+                    g.remote_dma(T["ql%d" % t][:, a:b].bitcast(dt.uint8), T.mq[:, a:b].bitcast(dt.uint8), T.sem[sc], T.sem.snd, pid, rid, m)
+                    g.wait_ge(T.sem[rs], got)
+                    g.remote_dma(T["sl%d" % t][:, a:b], T.ms[:, a:b], T.sem[ss], T.sem.snd, pid, rid, m)
+                    sent += 2 * nbits(m)
+            if core == rl[0]:
                 k = ES[t] // 2
-                g.wait_ge(T.sem.mi, len(topo.engines(src, core)))
+                g.wait_ge(T.sem.mi, got)
                 g.remote_dma(T["li%d" % t][:, 0:k], T.ml[:, 0:k], T.sem["ls%d" % t], T.sem.snd, pid, rid, m)
                 sent += nbits(m)
-            g.wait_ge(T.sem.snd, sent)
+            if sent:
+                g.wait_ge(T.sem.snd, sent)
 
 
 def clash(seen, outs, ins):
@@ -149,7 +152,7 @@ def deal(calls):
         slots = taken.setdefault(calls[i][0], [])
         k = 0
         for k, (a, b) in enumerate(slots + [(1e9, 1e9)]):
-            if at + calls[i][3] <= a + LOOK:
+            if at + calls[i][3] <= a:
                 break
             at = max(at, b)
         if calls[i][0]:
@@ -244,6 +247,12 @@ def rank_program(g, core, T, topo):
             kw["accum_out"] = ap(accum)
         run("S", [o, accum], [i, bias, scale], lambda: g.scalar.activation(ap(o), ap(i), fn, **kw))
 
+    def times(on_vector, o, i, c):
+        if on_vector:
+            ts(o, i, c, A.mult)
+        else:
+            act(o, i, F.Copy, scale=c)
+
     def mm(ps, lq, ls, la, rq, rs, a, b):
         us = 1.2 * CY * (b - a + 16)
         add("P", [R(ps)], [R(lq, la, la + 128), R(ls, la, la + 128), R(rq, a, b), R(rs, a, b)], us, us, "run",
@@ -290,8 +299,10 @@ def rank_program(g, core, T, topo):
     iota(R("jm"), [[0, 5], [1, 16]], 0)
     ms(R("ones"), 1.0)
     run("G", [R("ft")], [R("ones", 0, 516)], lambda: g.affine_select(T.ft[:], T.ones[:, 0:516], [[-1, 516]], A.is_equal, 0.0, 3, 4), 2.0, 0.17)
+    calls[-1][9] = EARLY
     for b in range(4):
         quant("qe", "se", 128 * b, 128 * b + 128, R("ft", 3 - b, 515 - b))
+        calls[-1][9] = EARLY
     ms(R("c0"), 0.0)
     ms(R("ve", 32, 48), 0.0)
     fill(R("ve", 32, 33), ES[0] + 2)
@@ -370,8 +381,7 @@ def rank_program(g, core, T, topo):
     quant("qu", "su", 0, 128, R("ut"))
     add("V", [R("qp")], [R("qu"), R("co", 2, 10)], 0.27, 0.27, "run",
         lambda: v.tensor_copy(T.qp[:].bitcast(dt.uint32), T.qu[:].bitcast(dt.uint32).indirect(T.co[:, 2:10])))
-    add("S", [R("sp")], [R("su"), R("co", 2, 10)], 0.27, 0.27, "run",
-        lambda: g.scalar.activation(T.sp[:], T.su[:].indirect(T.co[:, 2:10]), F.Copy))
+    add("V", [R("sp")], [R("su"), R("co", 2, 10)], 0.27, 0.27, "run", lambda: v.tensor_copy(T.sp[:], T.su[:].indirect(T.co[:, 2:10])))
     quant("qx0", "sx0", 0, H, R("xw0", 0, 4 * H))
     quant("qx0", "sx0", H, C, R("xw0", 4 * H, 4 * C))
     quant("qv", "sv", 0, 128, R("vt"))
@@ -383,7 +393,7 @@ def rank_program(g, core, T, topo):
     wrap16(R("p0"), R("c0", 0, 32))
     ts(R("pu", 0, 2), R("p0", 15, 32, 16), O16, A.subtract)
     cp(I(R("rs", 0, C), R("pu", 0, 2)), R("nb"))
-    act(R("rs", C, 2 * C), R("rs", 0, C), F.Copy, scale=-1.0)
+    ts(R("rs", C, 2 * C), R("rs", 0, C), -1.0, A.mult)
 
     def start(t, a=0, b=48):
         return R("c0", a, b) if t == 0 else R("cu", 48 * (t - 1) + a, 48 * (t - 1) + b)
@@ -401,6 +411,7 @@ def rank_program(g, core, T, topo):
             act(Rt("st", t, 80, 80 + E), n, F.Sign)
             tt(Rt("st", t, 160, 160 + E), e, Rt("st", t, 80, 80 + E), A.mult)
         tt(Rt("st", t, 160 + E, 160 + 2 * E), e, Rt("st", t, 80 + E, 80 + 2 * E), A.mult)
+        tt(Rt("st", t, 320, 320 + E), Rt("st", t, 320, 320 + E), Rt("st", t, 160, 160 + E), A.subtract)
         act(Rt("st", t, 240, 240 + E), Rt("st", t, 160, 160 + E), F.Identity, bias=C + 1.0)
         act(Rt("st", t, 240 + E, 240 + 2 * E), Rt("st", t, 160 + E, 160 + 2 * E), F.Identity, bias=PB + C + 1.0)
         wrap16(Rt("w80", t, 0, 2 * E), Rt("st", t, 240, 240 + 2 * E))
@@ -434,7 +445,7 @@ def rank_program(g, core, T, topo):
         wrap16(R("pw", k, k + 48), R("px", k, k + 48))
         ts(Rt("pu", t, 0, 3), R("pw", k + 15, k + 48, 16), O16, A.subtract)
         cp(I(Rt("wi", t), Rt("pu", t, 0, 3)), R("sid") if t == 1 else R("ids"))
-        act(Rt("rs", t, 0, C), Rt("wi", t, 0, C), F.Copy, scale=-BIG / 64)
+        times("rs" in ONV[t - 1], Rt("rs", t, 0, C), Rt("wi", t, 0, C), -BIG / 64)
         if t < 3:
             act(Rt("rs", t, C, 2 * C), Rt("wi", t, 0, C), F.Copy, scale=BIG / 64)
             ends(t)
@@ -450,52 +461,36 @@ def rank_program(g, core, T, topo):
         scan(Rt("ed", t), Rt("rs", t + 1, 0, C), Rt("wi", t + 1, 0, C), 0.0, A.add, A.max)
         scan(Rt("eb", t), R("m16s"), Rt("ed", t), 0.0, A.add, A.max)
         ts(Rt("ei", t), Rt("eb", t, 15, C, 16), O16B, A.subtract)
-        act(Rt("sg", t), I(Rt("sh", t), Rt("ei", t)), F.Copy)
+        if "sg" in ONV[t]:
+            cp(Rt("sg", t), I(Rt("sh", t), Rt("ei", t)))
+        else:
+            act(Rt("sg", t), I(Rt("sh", t), Rt("ei", t)), F.Copy)
         wrap4(Rt("ew", t), Rt("sg", t))
         tt(Rt("cw", t), Rt("ew", t, 3, C, 4), R("qc"), A.add)
 
     sent = [0]
 
-    def send_x(t):
+    def send_x(t, j):
         dst = T.cores[rank ^ STEP[t]]
-        qx, sx = "qx%d" % t, "sx%d" % t
+        a, b, sc, ss, rc, rs = pieces(t)[j]
+        qx, sx, lq, ls = "qx%d" % t, "sx%d" % t, "ql%d" % t, "sl%d" % t
         if topo.may_write(core, dst):
-            rid, pid = topo.addr(dst, core)
-            m = topo.mask(core, dst)
-
-            def f():
-                g.remote_dma(T["ql%d" % t][:].bitcast(dt.uint8), T[qx][:].bitcast(dt.uint8), T.sem["qc%d" % t], T.sem.snd, pid, rid, m)
-                g.remote_dma(T["sl%d" % t][:], T[sx][:], T.sem["qs%d" % t], T.sem.snd, pid, rid, m)
-            sent[0] += 2 * nbits(m)
-            got = nbits(topo.mask(dst, core))
+            to, frm, lands = dst, dst, (lq, ls, sc, ss)
         else:
-            rl = relays_of(core, dst, T, topo)
-            both = []
-            for codes in (True, False):
-                tr = []
-                for j, c in enumerate(rl):
-                    a, b = pieces(len(rl))[j]
-                    en = topo.engines(core, c)
-                    k = len(en) // len(rl)
-                    m = sum(1 << e for e in en[j * k:j * k + k])
-                    rid, pid = topo.addr(c, core)
-                    if codes:
-                        tr.append(RemoteDMATransfer(dst_ids=[DstId(rid=rid, pnc=pid)], dma_engine_mask=m, remote_sem=T.sem.mc,
-                                                    src=T[qx][:, a:b].bitcast(dt.uint8), dst=T.mq[:, a:b].bitcast(dt.uint8)))
-                    else:
-                        tr.append(RemoteDMATransfer(dst_ids=[DstId(rid=rid, pnc=pid)], dma_engine_mask=m, remote_sem=T.sem.mp,
-                                                    src=T[sx][:, a:b], dst=T.ms[:, a:b]))
-                    sent[0] += k
-                both.append(tr)
+            out, back = relays_of(core, dst, T, topo), relays_of(dst, core, T, topo)
+            to, frm, lands = out[j % len(out)], back[j % len(back)], ("mq", "ms", rc, rs)
+        rid, pid = topo.addr(to, core)
+        m = topo.mask(core, to)
 
-            def f():
-                for tr in both:
-                    g.remote_dma_fused(tr, local_sem=T.sem.snd)
-            got = sum(nbits(topo.mask(c, core)) for c in relays_of(dst, core, T, topo))
-        gone = (None, [("gx%d" % t, 0, 1)])
-        add("G", [gone], [R(qx), R(sx)], 0.6, HOP_X[t], "send", f)
-        add(None, [R("ql%d" % t)], [gone], 0.0, 0.0, "land", None, "qc%d" % t, got)
-        add(None, [R("sl%d" % t)], [gone], 0.0, 0.0, "land", None, "qs%d" % t, got)
+        def f():
+            g.remote_dma(T[lands[0]][:, a:b].bitcast(dt.uint8), T[qx][:, a:b].bitcast(dt.uint8), T.sem[lands[2]], T.sem.snd, pid, rid, m)
+            g.remote_dma(T[lands[1]][:, a:b], T[sx][:, a:b], T.sem[lands[3]], T.sem.snd, pid, rid, m)
+        sent[0] += 2 * nbits(m)
+        got = nbits(topo.mask(frm, core))
+        gone = (None, [("gx%d%d" % (t, j), 0, 1)])
+        add("G", [gone], [R(qx, a, b), R(sx, a, b)], 0.6 if t or j else FIRST, HOP_X[t], "send", f)
+        add(None, [R(lq, a, b)], [gone], 0.0, 0.0, "land", None, sc, got)
+        add(None, [R(ls, a, b)], [gone], 0.0, 0.0, "land", None, ss, got)
 
     def send_list(t):
         dst = T.cores[rank ^ STEP[t]]
@@ -518,7 +513,8 @@ def rank_program(g, core, T, topo):
         eo, of, cw = Rt("eo", t, 0, K), R("of%d" % t, 0, E // 2), Rt("cw", t)
         mm("ps0", "qp", "sp", 0, "qx%d" % t, "sx%d" % t, 0, H)
         mm("ps5", "qp", "sp", 0, "qx%d" % t, "sx%d" % t, H, C)
-        send_x(t)
+        for j in range(len(pieces(t))):
+            send_x(t, j)
         two = [(0, H, R("ps0", 0, H)), (H, C, R("ps5", 0, C - H))]
         for a, b, s in two:
             scan(R("pmm", 1 + a, 1 + b), Rt("rs", t, a, b), s, R("pmm", a, a + 1) if a else 0.0, A.add, A.max)
@@ -537,7 +533,7 @@ def rank_program(g, core, T, topo):
         scan(R("dist"), R("ones"), R("nrec"), 0.0, A.add, A.mult)
         tt(R("dg", 0, 2 * E), I(R("dist"), eo), Rt("st", t, 0, 2 * E), A.min)
         tt(R("ix", 0, 2 * E), Rt("st", t, 160, 160 + 2 * E), R("dg", 0, 2 * E), A.subtract)
-        tt(R("tt", 0, E), Rt("st", t, 320, 320 + E), R("ix", 0, E), A.subtract)
+        tt(R("tt", 0, E), Rt("st", t, 320, 320 + E), R("dg", 0, E), A.add)
         tt(R("ix", E, 2 * E), R("ix", E, 2 * E), R("tt", 0, E), A.max)
         scan(R("rk", 0, L * len(bl)), R("w%d" % E), R(sq), 0.0, A.mult, A.add)
         if E == 32:
@@ -549,10 +545,7 @@ def rank_program(g, core, T, topo):
         wrap4(R("sw", 0, 2 * E), R("sr", 0, 2 * E))
         ts(of, R("sw", 3, 2 * E, 4), 4.0, A.mult, C4, A.add)
         send_list(t)
-        if "ah" in ONV[t]:
-            ts(R("ah", 0, 8 * E), I(R(xw, 0, 4 * GC), of), 0.5, A.mult)
-        else:
-            act(R("ah", 0, 8 * E), I(R(xw, 0, 4 * GC), of), F.Copy, scale=0.5)
+        times("ah" in ONV[t], R("ah", 0, 8 * E), I(R(xw, 0, 4 * GC), of), 0.5)
         act(R("aa", 0, 8 * E), R("ah", 0, 8 * E), F.Copy, scale=2.0)
         tt(R("lh", 0, E), R("ix", 0, E), R("ix", E, 2 * E), A.min)
         tt(R("lh", 48, 48 + E), R("ix", 0, E), R("ix", E, 2 * E), A.max)
@@ -568,13 +561,11 @@ def rank_program(g, core, T, topo):
         tt(R("c3"), R("c1"), cw, A.add)
         tt(R("c4"), R("c3"), R("c2"), A.add)
         ts(R("eo4"), R("c4"), 4.0, A.mult, C4, A.add)
-        for b in range(4):
-            mm("ps%d" % (1 + b), "qe", "se", 128 * b, "ql%d" % t, "sl%d" % t, 0, C)
-            o = As(R("dh", b, 4 * C, 4), "dh", C * b, C * b + C)
-            if "dh" in ONV[t] and b % 2:
-                ts(o, R("ps%d" % (1 + b), 0, C), 0.5, A.mult)
-            else:
-                act(o, R("ps%d" % (1 + b), 0, C), F.Copy, scale=0.5)
+        for p in pieces(t):
+            for b in range(4):
+                mm("ps%d" % (1 + b), "qe", "se", 128 * b, "ql%d" % t, "sl%d" % t, p[0], p[1])
+                times("dh" in ONV[t] and b % 2, As(R("dh", 4 * p[0] + b, 4 * p[1], 4), "dh", C * b + p[0], C * b + p[1]),
+                      R("ps%d" % (1 + b), 0, p[1] - p[0]), 0.5)
         tt(R("mt", 0, 8 * E), I(R("dh"), R("li%d" % t, 0, E // 2)), R("ah", 0, 8 * E), A.add)
         quant("qm", "sm", 0, 128, R("mt"))
         for b in range(4):

from concourse.mybir import dt, AluOpType, ActivationFunctionType

C = 288
ES = [32, 40, 40]
STEP = [1, 2, 4]
GC = C + 2
XW = 4 * (GC + 80)
PB = 296
BIG = 2.0 ** 96
KV = 32
SPLIT = [False, True, False]
ONV = [("rs", "sg"), ("ah", "dh", "rs"), ("ah", "lo", "rs")]
CY, WAKE, LEAD, EARLY, FIRST = 0.00104, 0.14, 0.6, 1.0, 1.8
HOP_LIST, HOP_X = [2.2, 4.6, 2.6], [3.2, 7.0, 4.4]

f32, bf, i32, u16, u8, q4 = "float32", "bfloat16", "int32", "uint16", "uint8", "float8_e4m3fn_x4"
SCRATCH = {}
PER = {"nr": 48, "wi": 336, "rs": 2 * C, "st": 360, "me": 48, "eo": 6, "ei": 18, "cw": 72, "gs": 48, "pu": 4,
       "ed": C, "eb": C, "ew": C, "sg": C, "sh": 48, "gl": 48, "t40": 40, "w80": 80}
PART = {}


def _sb(name, n, d):
    SCRATCH[name] = ("sbuf", [128, n], d)


def _parts(name, d, parts):
    at = 0
    for n, w in parts:
        PART[n] = (name, at, w)
        at += (w + 15) // 16 * 16
    _sb(name, at, d)


for _t in range(4):
    _sb("xw%d" % _t, XW, bf)
    _sb("qx%d" % _t, C, q4)
    _sb("sx%d" % _t, C, u8)
for _t in range(3):
    _sb("ql%d" % _t, C, q4)
    _sb("sl%d" % _t, C, u8)
    _sb("of%d" % _t, 20, u16)
    _sb("li%d" % _t, 20, u16)
for _n, _k, _d in [("nr", 4, f32), ("wi", 4, bf), ("rs", 4, bf), ("st", 3, f32), ("me", 4, f32), ("eo", 3, u16), ("ei", 3, u16),
                   ("cw", 3, f32), ("gs", 3, f32), ("pu", 4, u16), ("ed", 3, bf), ("eb", 3, bf), ("ew", 3, f32), ("sg", 3, f32),
                   ("sh", 3, f32), ("gl", 3, f32), ("t40", 3, f32), ("w80", 3, f32)]:
    _sb(_n, _k * PER[_n], _d)
for _n, _w, _d in [
    ("mq", C, q4), ("ms", C, u8), ("ml", 20, u16),
    ("ut", 512, bf), ("vt", 512, bf), ("qu", 128, q4), ("su", 128, u8), ("qp", 128, q4), ("sp", 128, u8),
    ("qv", 128, q4), ("sv", 128, u8), ("wq", 512, q4), ("wp", 512, u8), ("qe", 512, q4), ("se", 512, u8),
    ("ft", 516, bf), ("ones", 592, bf), ("mt", 512, bf), ("qm", 128, q4), ("sm", 128, u8),
    ("dh", 4 * GC, bf), ("ah", 320, bf), ("aa", 320, bf), ("rt", 320, f32), ("yt", C, f32),
    ("pmm", 592, f32), ("nrec", 592, bf), ("dist", 592, bf), ("pi", 8, i32), ("zi", 8, i32), ("co", 52, u16), ("eo4", 72, u16),
    ("ro", 6, u16), ("kr", 4, u16), ("inv", 4, u16),
]:
    _sb(_n, _w, _d)
_parts("cf", f32, [("col", 16), ("jr", 72), ("jm", 80), ("tab", 64), ("md32", 64), ("md40", 80), ("kp32", 64), ("kp40", 80), ("qc", 72),
                   ("kc", 48), ("dd", 144)])
_parts("cb", bf, [("m16", 144), ("m16s", C), ("m4", C), ("ids", 48), ("nb", 32), ("w32", 260), ("w40", 486)])
_parts("lf", f32, [("vm", 80), ("vw", 80), ("vr", 80), ("dg", 80), ("ix", 80), ("tt", 40), ("sr", 80), ("sw", 80), ("lh", 96), ("lg", 2 * C),
                   ("lw", 2 * C), ("c1", 72), ("c2", 72), ("c3", 72), ("c4", 72)])
_parts("lb", bf, [("sq32", 260), ("sq40", 486), ("rk", 486), ("kj", 144), ("kk", 96), ("sid", 48)])
_parts("zf", f32, [("zb", 64), ("zt", 64), ("ve", 48), ("cn", 8), ("c0", 48), ("cu", 144), ("ky", 48), ("kw", 48), ("kx", 48), ("kb", 4),
                   ("ka", 4), ("po", 48), ("p0", 32), ("pw", 144), ("zz", 144), ("px", 144)])
for _t in range(6):
    SCRATCH["ps%d" % _t] = ("psum", [128, 512], f32)

SEMAPHORES = ["V", "S", "P", "G", "ldz", "ldx", "ldy", "ldu", "ldv", "ldw", "ldp", "sty", "stw", "stc", "std", "sts", "stz", "snd",
              "qc0", "qc1", "qc2", "qs0", "qs1", "qs2", "ls0", "ls1", "ls2", "qd0", "qd1", "qd2", "qt0", "qt1", "qt2",
              "mc", "mp", "md", "mr", "mi"]

A = AluOpType
F = ActivationFunctionType


def nbits(m):
    return bin(m).count("1")


def relays_of(src, dst, T, topo):
    return [c for c in topo.cores_of(src) if c != src and T.rank_of(c) is None and topo.die(c) == topo.die(src) and topo.may_write(c, dst)]


def pieces(t):
    p = [(0, 4 * KV), (4 * KV, C)] if SPLIT[t] else [(0, C)]
    return [(a, b, "q%s%d" % ("cd"[j], t), "q%s%d" % ("st"[j], t), "m" + "cd"[j], "m" + "pr"[j]) for j, (a, b) in enumerate(p)]


def relay_program(g, core, T, topo):
    for r, src in enumerate(T.cores):
        for t in range(3):
            dst = T.cores[r ^ STEP[t]]
            if topo.may_write(src, dst):
                continue
            rl = relays_of(src, dst, T, topo)
            if core not in rl:
                continue
            got = nbits(topo.mask(src, core))
            rid, pid = topo.addr(dst, core)
            m = topo.mask(core, dst)
            sent = 0
            for j, (a, b, sc, ss, rc, rs) in enumerate(pieces(t)):
                if rl[j % len(rl)] == core:
                    g.wait_ge(T.sem[rc], got)
                    g.remote_dma(T["ql%d" % t][:, a:b].bitcast(dt.uint8), T.mq[:, a:b].bitcast(dt.uint8), T.sem[sc], T.sem.snd, pid, rid, m)
                    g.wait_ge(T.sem[rs], got)
                    g.remote_dma(T["sl%d" % t][:, a:b], T.ms[:, a:b], T.sem[ss], T.sem.snd, pid, rid, m)
                    sent += 2 * nbits(m)
            if core == rl[0]:
                k = ES[t] // 2
                g.wait_ge(T.sem.mi, got)
                g.remote_dma(T["li%d" % t][:, 0:k], T.ml[:, 0:k], T.sem["ls%d" % t], T.sem.snd, pid, rid, m)
                sent += nbits(m)
            if sent:
                g.wait_ge(T.sem.snd, sent)


def clash(seen, outs, ins):
    for regs, w in ((outs, True), (ins, False)):
        for name, a, b in regs:
            for lo, hi, wr, who in seen.get(name, []):
                if lo < b and a < hi and (w or wr):
                    yield who


def enter(seen, outs, ins, who):
    for regs, w in ((ins, False), (outs, True)):
        for name, a, b in regs:
            l = seen.setdefault(name, [])
            if w:
                l[:] = [e for e in l if not (a <= e[0] and e[1] <= b)]
            l.append((a, b, w, who))


def deal(calls):
    seen, before, after = {}, [], [[] for c in calls]
    for i, c in enumerate(calls):
        before.append(set(clash(seen, c[1], c[2])))
        enter(seen, c[1], c[2], i)
        for j in before[i]:
            after[j].append(i)
    chain = [0.0] * len(calls)
    for i in reversed(range(len(calls))):
        chain[i] = calls[i][4] + calls[i][9] + max([WAKE + chain[j] for j in after[i]] + [0.0])
    gate = [i for i, c in enumerate(calls) if c[1] and c[1][0][0] == "gl0"][0]
    taken, begin = {}, [0.0] * len(calls)
    for i in sorted(range(len(calls)), key=lambda i: -chain[i]):
        at = max([begin[k] + calls[k][4] + WAKE for k in before[i]] + [0.0])
        if calls[i][7] is True:
            at = max(at, begin[gate] + calls[gate][3])
        slots = taken.setdefault(calls[i][0], [])
        k = 0
        for k, (a, b) in enumerate(slots + [(1e9, 1e9)]):
            if at + calls[i][3] <= a:
                break
            at = max(at, b)
        if calls[i][0]:
            slots.insert(k, (at, at + calls[i][3]))
        begin[i] = at
    return [calls[i] for i in sorted(range(len(calls)), key=lambda i: (begin[i], -chain[i]))]


def rank_program(g, core, T, topo):
    rank = T.rank_of(core)
    if rank is None:
        relay_program(g, core, T, topo)
        return
    Q = {"V": g.vector, "S": g.scalar, "P": g.tensor, "G": g, "Y": g.sync}
    calls = []

    def R(name, a=0, b=None, s=1):
        buf, at, w = PART.get(name, (name, 0, SCRATCH[name][1][1] if name in SCRATCH else 0))
        b = w if b is None else b
        ap = T[buf][:, at + a:at + b] if s == 1 else T[buf][:, at + a:at + b:s]
        return (ap, [(name, a, b)], (b - a + s - 1) // s, 2 if SCRATCH[buf][2] == bf else 4)

    def Rt(name, t, a=0, b=None, s=1):
        return R(name, PER[name] * t + a, PER[name] * t + (PER[name] if b is None else b), s)

    def As(x, name, a, b):
        return (x[0], [(name, a, b)], x[2], x[3])

    def I(win, off):
        return (win[0].indirect(off[0]), win[1] + off[1], 16 * off[2], win[3], off[1])

    def ap(x):
        return x[0] if isinstance(x, tuple) else x

    def add(q, outs, ins, busy, done, kind, f, sem=None, n=0):
        o, i = [], [e for x in ins if isinstance(x, tuple) for e in x[1]]
        for x in outs:
            if isinstance(x, tuple):
                i = i + (x[4] if len(x) == 5 else [])
                o = o + (x[1][:1] if len(x) == 5 else x[1])
        i = [(e[0], 0, 512) if e[0].startswith("ps") else e for e in i]
        calls.append([q, o, i, busy, done, kind, f, sem, n, 0.0])

    def run(q, outs, ins, f, cy=1.0, fix=0.0):
        o, x = outs[0], ins[0] if ins else outs[0]
        if len(o) == 5:
            us = 0.05 + 3.8 * CY * o[2]
        elif len(x) == 5:
            us = 0.06 + 1.56 * CY * x[2]
        elif fix:
            us = fix + cy * CY * o[2]
        else:
            us = CY * max(64, cy * o[2])
        add(q, outs, ins, us, us, "run", f)

    def dma(q, sem, out, in_, us, n=16, also=()):
        add(q, [out], [in_] + list(also), 0.05, us, "dma", lambda: Q[q].dma_start(ap(out), ap(in_)), sem, n)

    v = g.vector

    def fast(*xs):
        return 0.5 if all(x[3] == 2 for x in xs) else 1.0

    def cp(o, i):
        run("V", [o], [i], lambda: v.tensor_copy(ap(o), ap(i)), fast(o, i))

    def ms(o, c):
        run("V", [o], [], lambda: v.memset(ap(o), c), fast(o))

    def tt(o, a, b, op):
        run("V", [o], [a, b], lambda: v.tensor_tensor(ap(o), ap(a), ap(b), op), 1.0 if b[1][0][0].startswith("ps") else 2.0)

    def ts(o, a, s1, op0, s2=None, op1=None):
        if op1 is None:
            run("V", [o], [a, s1], lambda: v.tensor_scalar(ap(o), ap(a), ap(s1), None, op0), fast(o, a))
        else:
            run("V", [o], [a, s1, s2], lambda: v.tensor_scalar(ap(o), ap(a), ap(s1), ap(s2), op0, op1), fast(o, a))

    def scan(o, d0, d1, init, op0, op1):
        run("V", [o], [d0, d1, init], lambda: v.tensor_tensor_scan(ap(o), ap(d0), ap(d1), ap(init), op0, op1), fast(o, d0, d1))

    def quant(qn, sn, a, b, src):
        run("V", [R(qn, a, b), R(sn, a, b)], [src], lambda: v.quantize_mx(T[qn][:, a:b], T[sn][:, a:b], ap(src)), 1.06, 0.015)

    def act(o, i, fn, bias=None, scale=None, accum=None):
        kw = {}
        if bias is not None:
            kw["bias"] = ap(bias)
        if scale is not None:
            kw["scale"] = ap(scale)
        if accum is not None:
            kw["accum_out"] = ap(accum)
        run("S", [o, accum], [i, bias, scale], lambda: g.scalar.activation(ap(o), ap(i), fn, **kw))

    def times(on_vector, o, i, c):
        if on_vector:
            ts(o, i, c, A.mult)
        else:
            act(o, i, F.Copy, scale=c)

    def mm(ps, lq, ls, la, rq, rs, a, b):
        us = 1.2 * CY * (b - a + 16)
        add("P", [R(ps)], [R(lq, la, la + 128), R(ls, la, la + 128), R(rq, a, b), R(rs, a, b)], us, us, "run",
            lambda: g.tensor.matmul_mx(T[ps][:, 0:b - a], T[lq][:, la:la + 128], T[ls][:, la:la + 128], T[rq][:, a:b], T[rs][:, a:b], True, True))

    def iota(o, pat, base, cm=0, small=True, late=False):
        if small:
            run("G", [o], [], lambda: g.iota(ap(o), pat, base, cm, allow_small_or_imprecise_dtypes=True), 2.0, 0.13)
            calls[-1][7] = late
        else:
            run("G", [o], [], lambda: g.iota(ap(o), pat, base, cm), 2.0, 0.13)

    def fill(o, c=0, late=False):
        iota(o, [[0, o[2]]], c, late=late)

    def wrap16(o, row):
        scan(o, R("m16", 0, row[2]), row, 0.0, A.add, A.max)

    def wrap4(o, row):
        scan(o, R("m4", 0, row[2]), row, 0.0, A.add, A.max)

    RC, R4, RM, P32, R1, R41, O16, C4, SA, SB, O16B, TMP, NR, R2 = [R("col", j, j + 1) for j in range(14)]

    def J(a, n):
        return R("jr", a, a + n)

    def blocks(E):
        if E == 32:
            return [(0, 0, 15, 1.0), (1, 0, 31, 1.0), (2, 1, 47, -1.0), (3, 1, 63, -1.0)]
        return [(0, 0, 15, 1.0), (1, 0, 31, 1.0), (2, 0, 39, SA), (2, 1, 47, SB), (3, 1, 63, -1.0), (4, 1, 79, -1.0)]

    H = 4 * KV
    dma("Y", "ldz", R("zi", 0, 2), T.z[:], 1.9)
    dma("S", "ldu", R("ut"), T.u[:], 2.6)
    dma("Y", "ldx", R("xw0", 0, 4 * H), T.x[:, 0:4 * H], 2.9)
    dma("Y", "ldy", R("xw0", 4 * H, 4 * C), T.x[:, 4 * H:4 * C], 3.4)
    x0 = [R("xw0", 0, 4 * C)]
    dma("Y", "ldw", (T.wq[:].bitcast(dt.uint8),) + R("wq")[1:], T.wc[:], 3.5, also=x0)
    dma("Y", "ldp", R("wp"), T.ws[:], 3.5, also=x0)
    dma("Y", "ldv", R("vt"), T.v[:], 3.5, also=x0)

    iota(R("pi", 0, 1), [[0, 1]], 0, 1, False)
    iota(R("jr"), [[1, 72]], 0)
    iota(R("jm"), [[0, 5], [1, 16]], 0)
    ms(R("ones"), 1.0)
    run("G", [R("ft")], [R("ones", 0, 516)], lambda: g.affine_select(T.ft[:], T.ones[:, 0:516], [[-1, 516]], A.is_equal, 0.0, 3, 4), 2.0, 0.17)
    calls[-1][9] = EARLY
    for b in range(4):
        quant("qe", "se", 128 * b, 128 * b + 128, R("ft", 3 - b, 515 - b))
        calls[-1][9] = EARLY
    ms(R("c0"), 0.0)
    ms(R("ve", 32, 48), 0.0)
    fill(R("ve", 32, 33), ES[0] + 2)
    fill(R("c0", 33, 34), C + ES[0])
    fill(R("cu", 0, 144, 48))
    for t in range(3):
        fill(R("xw%d" % t, 4 * C, 4 * GC), late=t > 0)
        fill(Rt("wi", t + 1), late=t > 0)
    fill(R("dh", 4 * C, 4 * GC))
    fill(R("lh", 32, 48))
    fill(R("lh", 80, 96))
    fill(R("mt", 256, 512), late=True)
    fill(R("gs", 48, 144), late=True)
    for t in (1, 2):
        iota(Rt("gs", t, 32 + 2 * t, 34 + 2 * t), [[ES[t], 2]], C)
    iota(R("dd"), [[0, 3], [1, 48]], C)
    iota(R("qc"), [[4, 72]], -C)
    ms(R("rs", 0, C), 0.0)
    ms(R("nb"), -BIG)
    fill(R("nrec", 0, 1))
    fill(R("nrec", C + 1, PB + 1))
    fill(R("nrec", PB + C + 1, 592))
    fill(R("pmm", 0, 1))
    ms(R("pmm", C + 1, PB + 1), -BIG)
    ms(R("pmm", PB + C + 1, 592), BIG)
    ts(R("pi", 1, 2), R("pi", 0, 1), 15, A.bitwise_and)
    ts(R("pi", 2, 3), R("pi", 0, 1), 2, A.arith_shift_right, 3, A.bitwise_and)
    ts(R("pi", 3, 4), R("pi", 0, 1), 3, A.bitwise_and)
    ts(R("pi", 4, 5), R("pi", 0, 1), 31, A.bitwise_and)
    cp(R("col", 0, 4), R("pi", 1, 5))
    act(R("col", 4, 6), R("col", 0, 2), F.Identity, bias=1.0)
    ts(R("co", 0, 2), J(0, 2), 32.0, A.mult, P32, A.add)
    ts(R("co", 2, 10), J(0, 8), 16.0, A.mult)
    ts(R("co", 10, 28), J(0, 18), 0.0, A.mult, RC, A.add)
    ts(R("co", 28, 46), J(0, 18), 0.0, A.mult, RM, A.add)
    ts(R("co", 46, 50), J(0, 4), 2.0, A.is_ge)
    ts(R("tab", 0, 16), J(0, 16), RC, A.is_equal, -4096.0, A.mult)
    ts(R("tab", 16, 32), J(0, 16), R1, A.is_equal, 1024.0, A.mult)
    tt(R("tab", 32, 48), R("tab", 0, 16), R("tab", 16, 32), A.add)
    ts(R("tab", 48, 52), J(0, 4), R4, A.is_equal, -4096.0, A.mult)
    ts(R("tab", 52, 56), J(0, 4), R41, A.is_equal, 1024.0, A.mult)
    tt(R("tab", 56, 60), R("tab", 48, 52), R("tab", 52, 56), A.add)
    ts(O16, RC, 15.0, A.is_lt, 1024.0, A.mult)
    ts(TMP, R4, 3.0, A.is_lt, -4096.0, A.mult)
    ts(C4, TMP, 4.0 * C, A.add, RM, A.add)
    ts(SA, RC, 8.0, A.is_lt)
    act(SB, SA, F.Identity, bias=-1.0)
    act(NR, RC, F.Copy, scale=-1.0)
    act(R2, RC, F.Copy, scale=2.0)
    act(O16B, O16, F.Identity, bias=1.0, scale=0.125)
    act(R("ids"), J(0, 48), F.Identity, bias=1.0)
    act(R("kc"), J(0, 48), F.Identity, bias=1.0, scale=-1.0 / 64)
    act(R("qc"), R("qc"), F.Identity, bias=R4)
    act(R("m16"), I(R("tab", 32, 48), R("co", 10, 19)), F.Copy)
    act(R("m16s"), I(R("tab", 32, 48), R("co", 10, 28)), F.Copy, scale=0.125)
    act(R("m4"), I(R("tab", 56, 60), R("co", 28, 46)), F.Copy)
    for E in (32, 40):
        L, w, sq, md = 2 * E + 1, "w%d" % E, "sq%d" % E, "md%d" % E
        iota(R(w), [[E % 16, 2], [-16, len(blocks(E)) // 2], [1, L]], 0, late=E == 40)
        act(R(w), R(w), F.Abs, bias=NR)
        act(R(w), R(w), F.Sign, bias=-0.5)
        act(R("kp%d" % E), R("jm", 0, 2 * E), F.Sign)
        ts(R(md, 0, E), R("jm", 0, E), RC, A.is_equal, -1.0, A.mult)
        ts(R(md, E, 2 * E), R("jm", E, 2 * E), RC, A.is_equal)
        if E == 32:
            act(R(sq, 2 * E, 4 * L, L), J(0, 4), F.Identity, bias=R2, scale=32.0)
            fill(R(w, 0, 4 * L, L))
        else:
            act(R(sq, 2 * E, 2 * L, L), J(0, 2), F.Identity, bias=R2, scale=32.0)
            act(R(sq, 4 * L - 1, 6 * L, L), J(2, 3), F.Identity, bias=R2, scale=32.0)
            fill(R(sq, 3 * L - 1, 3 * L), late=True)
            fill(R("kp40", E, E + 1), late=True)
            fill(R(w, 0, 3 * L, L))
            fill(R(w, 4 * L, 6 * L, L))

    quant("qu", "su", 0, 128, R("ut"))
    add("V", [R("qp")], [R("qu"), R("co", 2, 10)], 0.27, 0.27, "run",
        lambda: v.tensor_copy(T.qp[:].bitcast(dt.uint32), T.qu[:].bitcast(dt.uint32).indirect(T.co[:, 2:10])))
    add("V", [R("sp")], [R("su"), R("co", 2, 10)], 0.27, 0.27, "run", lambda: v.tensor_copy(T.sp[:], T.su[:].indirect(T.co[:, 2:10])))
    quant("qx0", "sx0", 0, H, R("xw0", 0, 4 * H))
    quant("qx0", "sx0", H, C, R("xw0", 4 * H, 4 * C))
    quant("qv", "sv", 0, 128, R("vt"))

    cp(R("zb"), I(R("zi", 0, 2), R("co", 46, 50)))
    run("V", [R("zt")], [R("zb")], lambda: v.transpose(ap(R("zt")), ap(R("zb"))))
    cp(R("ve", 0, 32), I(R("zt"), R("co", 0, 2)))
    scan(R("c0", 1, 33), R("ones", 0, 32), R("ve", 0, 32), 0.0, A.mult, A.add)
    wrap16(R("p0"), R("c0", 0, 32))
    ts(R("pu", 0, 2), R("p0", 15, 32, 16), O16, A.subtract)
    cp(I(R("rs", 0, C), R("pu", 0, 2)), R("nb"))
    ts(R("rs", C, 2 * C), R("rs", 0, C), -1.0, A.mult)

    def start(t, a=0, b=48):
        return R("c0", a, b) if t == 0 else R("cu", 48 * (t - 1) + a, 48 * (t - 1) + b)

    def ends(t):
        E = ES[t]
        n = R("ve", 0, E) if t == 0 else Rt("nr", t, 0, E)
        act(Rt("st", t, 0, E), n, F.Relu, bias=-1.0)
        act(Rt("st", t, 80 + E, 80 + 2 * E), Rt("st", t, 0, E), F.Sign, accum=R("cn", 1, 2) if t == 0 else None)
        act(Rt("st", t, E, 2 * E), n, F.Relu, bias=-1.0)
        e = Rt("st", t, 160, 160 + E) if t == 0 else Rt("t40", t, 0, E)
        act(e, start(t, 1, 1 + E), F.Identity, bias=-(C + 1.0))
        act(Rt("st", t, 320, 320 + E), start(t, 0, E), F.Identity, bias=1.0 - 2 * C, scale=2.0)
        if t:
            act(Rt("st", t, 80, 80 + E), n, F.Sign)
            tt(Rt("st", t, 160, 160 + E), e, Rt("st", t, 80, 80 + E), A.mult)
        tt(Rt("st", t, 160 + E, 160 + 2 * E), e, Rt("st", t, 80 + E, 80 + 2 * E), A.mult)
        tt(Rt("st", t, 320, 320 + E), Rt("st", t, 320, 320 + E), Rt("st", t, 160, 160 + E), A.subtract)
        act(Rt("st", t, 240, 240 + E), Rt("st", t, 160, 160 + E), F.Identity, bias=C + 1.0)
        act(Rt("st", t, 240 + E, 240 + 2 * E), Rt("st", t, 160 + E, 160 + 2 * E), F.Identity, bias=PB + C + 1.0)
        wrap16(Rt("w80", t, 0, 2 * E), Rt("st", t, 240, 240 + 2 * E))
        ts(Rt("eo", t, 0, E // 8), Rt("w80", t, 15, 2 * E, 16), O16, A.subtract)

    ends(0)
    act(R("ve", 33, 34), R("cn", 1, 2), F.Identity, bias=2.0)
    for t in (1, 2, 3):
        act(Rt("me", t), R("ve"), F.Relu, bias=-2.0 * t)
        if t < 3:
            act(Rt("me", 0), R("ve"), F.Relu, bias=-2.0 * t - 1)
            act(R("kk", 0, 48), Rt("me", t), F.Sign, accum=R("cn", 2 * t, 2 * t + 1))
            act(R("kk", 48, 96), Rt("me", 0), F.Sign, accum=R("cn", 2 * t + 1, 2 * t + 2))
            act(R("ve", 32 + 2 * t, 34 + 2 * t), R("cn", 2 * t, 2 * t + 2), F.Identity, bias=2.0 * t + 2)
    tt(R("ky"), R("ve"), R("kc"), A.add)
    wrap16(R("kw"), R("ky"))
    ts(R("kb", 0, 3), R("kw", 15, 48, 16), -1.0, A.mult, O16, A.add)
    for k in range(3):
        act(R("kj", 48 * k, 48 * k + 48), R("ky"), F.Sign, bias=R("kb", k, k + 1), accum=R("ka", k, k + 1))
    ts(R("kr", 0, 3), R("ka", 0, 3), 0.5, A.mult, 23.5, A.add)
    cp(I(R("sid"), R("kr", 0, 3)), R("ids"))
    wrap16(R("kx"), R("sid"))
    ts(R("inv", 0, 3), R("kx", 15, 48, 16), O16, A.subtract, -1.0, A.add)
    for t in (1, 2, 3):
        k = 48 * (t - 1)
        act(Rt("nr", t), I(Rt("me", t), R("inv", 0, 3)), F.Copy)
        scan(R("cu", k + 1, k + 48), R("ones", 0, 47), Rt("nr", t, 0, 47), 0.0, A.mult, A.add)
        act(R("zz", k, k + 48), Rt("nr", t), F.Copy, scale=-1000.0)
        tt(R("zz", k, k + 48), R("zz", k, k + 48), R("dd", k, k + 48), A.add)
        tt(R("px", k, k + 48), R("zz", k, k + 48), start(t), A.max)
        wrap16(R("pw", k, k + 48), R("px", k, k + 48))
        ts(Rt("pu", t, 0, 3), R("pw", k + 15, k + 48, 16), O16, A.subtract)
        cp(I(Rt("wi", t), Rt("pu", t, 0, 3)), R("sid") if t == 1 else R("ids"))
        times("rs" in ONV[t - 1], Rt("rs", t, 0, C), Rt("wi", t, 0, C), -BIG / 64)
        if t < 3:
            act(Rt("rs", t, C, 2 * C), Rt("wi", t, 0, C), F.Copy, scale=BIG / 64)
            ends(t)
    dma("Y", "stz", T.oz[:], (T.nr[0:128:16, 3 * 48:3 * 48 + 40],) + Rt("nr", 3)[1:], 2.0)
    act(R("po"), I(start(1), R("kr", 0, 3)), F.Copy)
    for t in range(3):
        if t == 0:
            tt(Rt("sh", 0), start(0), R("po"), A.subtract)
        else:
            act(Rt("gl", t), I(Rt("gs", t), R("inv", 0, 3)), F.Copy)
            tt(Rt("gl", t), Rt("gl", t), start(t), A.max)
            tt(Rt("sh", t), Rt("gl", t), start(t + 1), A.subtract)
        scan(Rt("ed", t), Rt("rs", t + 1, 0, C), Rt("wi", t + 1, 0, C), 0.0, A.add, A.max)
        scan(Rt("eb", t), R("m16s"), Rt("ed", t), 0.0, A.add, A.max)
        ts(Rt("ei", t), Rt("eb", t, 15, C, 16), O16B, A.subtract)
        if "sg" in ONV[t]:
            cp(Rt("sg", t), I(Rt("sh", t), Rt("ei", t)))
        else:
            act(Rt("sg", t), I(Rt("sh", t), Rt("ei", t)), F.Copy)
        wrap4(Rt("ew", t), Rt("sg", t))
        tt(Rt("cw", t), Rt("ew", t, 3, C, 4), R("qc"), A.add)

    sent = [0]

    def send_x(t, j):
        dst = T.cores[rank ^ STEP[t]]
        a, b, sc, ss, rc, rs = pieces(t)[j]
        qx, sx, lq, ls = "qx%d" % t, "sx%d" % t, "ql%d" % t, "sl%d" % t
        if topo.may_write(core, dst):
            to, frm, lands = dst, dst, (lq, ls, sc, ss)
        else:
            out, back = relays_of(core, dst, T, topo), relays_of(dst, core, T, topo)
            to, frm, lands = out[j % len(out)], back[j % len(back)], ("mq", "ms", rc, rs)
        rid, pid = topo.addr(to, core)
        m = topo.mask(core, to)

        def f():
            g.remote_dma(T[lands[0]][:, a:b].bitcast(dt.uint8), T[qx][:, a:b].bitcast(dt.uint8), T.sem[lands[2]], T.sem.snd, pid, rid, m)
            g.remote_dma(T[lands[1]][:, a:b], T[sx][:, a:b], T.sem[lands[3]], T.sem.snd, pid, rid, m)
        sent[0] += 2 * nbits(m)
        got = nbits(topo.mask(frm, core))
        gone = (None, [("gx%d%d" % (t, j), 0, 1)])
        add("G", [gone], [R(qx, a, b), R(sx, a, b)], 0.6 if t or j else FIRST, HOP_X[t], "send", f)
        add(None, [R(lq, a, b)], [gone], 0.0, 0.0, "land", None, sc, got)
        add(None, [R(ls, a, b)], [gone], 0.0, 0.0, "land", None, ss, got)

    def send_list(t):
        dst = T.cores[rank ^ STEP[t]]
        k = ES[t] // 2
        if topo.may_write(core, dst):
            to, land, sem, frm = dst, "li%d" % t, "ls%d" % t, dst
        else:
            to, land, sem, frm = relays_of(core, dst, T, topo)[0], "ml", "mi", relays_of(dst, core, T, topo)[0]
        rid, pid = topo.addr(to, core)
        m = topo.mask(core, to)
        sent[0] += nbits(m)
        gone = (None, [("gl%d" % t, 0, 1)])
        add("G", [gone], [R("of%d" % t, 0, k)], 0.3, HOP_LIST[t], "send",
            lambda: g.remote_dma(T[land][:, 0:k], T["of%d" % t][:, 0:k], T.sem[sem], T.sem.snd, pid, rid, m))
        add(None, [R("li%d" % t, 0, k)], [gone], 0.0, 0.0, "land", None, "ls%d" % t, nbits(topo.mask(frm, core)))

    for t in range(3):
        E, xw = ES[t], "xw%d" % t
        L, bl, sq, K = 2 * E + 1, blocks(E), "sq%d" % E, E // 8
        eo, of, cw = Rt("eo", t, 0, K), R("of%d" % t, 0, E // 2), Rt("cw", t)
        mm("ps0", "qp", "sp", 0, "qx%d" % t, "sx%d" % t, 0, H)
        mm("ps5", "qp", "sp", 0, "qx%d" % t, "sx%d" % t, H, C)
        for j in range(len(pieces(t))):
            send_x(t, j)
        two = [(0, H, R("ps0", 0, H)), (H, C, R("ps5", 0, C - H))]
        for a, b, s in two:
            scan(R("pmm", 1 + a, 1 + b), Rt("rs", t, a, b), s, R("pmm", a, a + 1) if a else 0.0, A.add, A.max)
            scan(R("pmm", PB + 1 + a, PB + 1 + b), Rt("rs", t, C + a, C + b), s, R("pmm", PB + a, PB + a + 1) if a else 0.0, A.add, A.min)
        tt(R("vm", 0, 2 * E), I(R("pmm"), eo), R("md%d" % E), A.mult)
        act(R("vr", 0, 2 * E), I(R("pmm"), eo), F.Copy)
        scan(R("vw", 0, 2 * E), R("kp%d" % E), R("vm", 0, 2 * E), 0.0, A.mult, A.add)
        calls[-1][9] = LEAD
        for j, (k, l, bc, sc) in enumerate(bl):
            act(R(sq, j * L + E, j * L + 2 * E), R("vr", l * E, l * E + E), F.Sign, bias=R("vw", bc, bc + 1), scale=sc)
        for j in range(len(bl)):
            act(R(sq, j * L, j * L + E), R(sq, j * L + E, j * L + 2 * E), F.Square)
        for a, b, s in two:
            tt(R("nrec", 1 + a, 1 + b), R("pmm", a, b), s, A.is_ge)
            tt(R("nrec", PB + 1 + a, PB + 1 + b), R("pmm", PB + a, PB + b), s, A.is_le)
        scan(R("dist"), R("ones"), R("nrec"), 0.0, A.add, A.mult)
        tt(R("dg", 0, 2 * E), I(R("dist"), eo), Rt("st", t, 0, 2 * E), A.min)
        tt(R("ix", 0, 2 * E), Rt("st", t, 160, 160 + 2 * E), R("dg", 0, 2 * E), A.subtract)
        tt(R("tt", 0, E), Rt("st", t, 320, 320 + E), R("dg", 0, E), A.add)
        tt(R("ix", E, 2 * E), R("ix", E, 2 * E), R("tt", 0, E), A.max)
        scan(R("rk", 0, L * len(bl)), R("w%d" % E), R(sq), 0.0, A.mult, A.add)
        if E == 32:
            ts(R("ro", 0, 4), R("rk", L - 1, 4 * L, L), 0.5, A.mult)
        else:
            ts(R("ro", 0, 2), R("rk", L - 1, 2 * L, L), 0.5, A.mult)
            ts(R("ro", 2, 5), R("rk", 4 * L - 1, 6 * L, L), 0.5, A.mult)
        cp(I(R("sr", 0, 2 * E), R("ro", 0, K)), R("ix", 0, 2 * E))
        wrap4(R("sw", 0, 2 * E), R("sr", 0, 2 * E))
        ts(of, R("sw", 3, 2 * E, 4), 4.0, A.mult, C4, A.add)
        send_list(t)
        times("ah" in ONV[t], R("ah", 0, 8 * E), I(R(xw, 0, 4 * GC), of), 0.5)
        act(R("aa", 0, 8 * E), R("ah", 0, 8 * E), F.Copy, scale=2.0)
        tt(R("lh", 0, E), R("ix", 0, E), R("ix", E, 2 * E), A.min)
        tt(R("lh", 48, 48 + E), R("ix", 0, E), R("ix", E, 2 * E), A.max)
        if "lo" in ONV[t]:
            cp(R("lg", 0, C), I(R("lh", 0, 48), Rt("ei", t)))
        else:
            act(R("lg", 0, C), I(R("lh", 0, 48), Rt("ei", t)), F.Copy)
        act(R("lg", C, 2 * C), I(R("lh", 48, 96), Rt("ei", t)), F.Identity, bias=-1.0)
        wrap4(R("lw", 0, C), R("lg", 0, C))
        wrap4(R("lw", C, 2 * C), R("lg", C, 2 * C))
        tt(R("c1"), R("lw", 3, C, 4), cw, A.is_le)
        tt(R("c2"), R("lw", C + 3, 2 * C, 4), cw, A.is_le)
        tt(R("c3"), R("c1"), cw, A.add)
        tt(R("c4"), R("c3"), R("c2"), A.add)
        ts(R("eo4"), R("c4"), 4.0, A.mult, C4, A.add)
        for p in pieces(t):
            for b in range(4):
                mm("ps%d" % (1 + b), "qe", "se", 128 * b, "ql%d" % t, "sl%d" % t, p[0], p[1])
                times("dh" in ONV[t] and b % 2, As(R("dh", 4 * p[0] + b, 4 * p[1], 4), "dh", C * b + p[0], C * b + p[1]),
                      R("ps%d" % (1 + b), 0, p[1] - p[0]), 0.5)
        tt(R("mt", 0, 8 * E), I(R("dh"), R("li%d" % t, 0, E // 2)), R("ah", 0, 8 * E), A.add)
        quant("qm", "sm", 0, 128, R("mt"))
        for b in range(4):
            mm("ps%d" % (1 + b), "wq", "wp", 128 * b, "qm", "sm", 0, 128)
            act(R("rt", 80 * b, 80 * b + 2 * E), R("ps%d" % (1 + b), 0, 2 * E), F.Relu, scale=0.03125)
            tt(As(R(xw, 4 * GC + b, 4 * GC + 8 * E, 4), xw, 4 * GC + 80 * b, 4 * GC + 80 * b + 80),
               R("rt", 80 * b, 80 * b + 2 * E), R("aa", b, 8 * E, 4), A.add)
        xn, win = "xw%d" % (t + 1), As(R(xw, 0, 4 * GC + 8 * E), xw, 0, XW)
        act(R(xn, 4 * H, 4 * C), I(win, R("eo4", KV, 72)), F.Copy)
        cp(R(xn, 0, 4 * H), I(win, R("eo4", 0, KV)))
        quant("qx%d" % (t + 1), "sx%d" % (t + 1), 0, H, R(xn, 0, 4 * H))
        quant("qx%d" % (t + 1), "sx%d" % (t + 1), H, C, R(xn, 4 * H, 4 * C))

    mm("ps0", "qv", "sv", 0, "qx3", "sx3", 0, H)
    mm("ps1", "qv", "sv", 0, "qx3", "sx3", H, C)
    act(R("yt", 0, H), R("ps0", 0, H), F.Copy)
    cp(R("yt", H, C), R("ps1", 0, C - H))
    dma("Y", "stc", T.oc[:, 0:4 * H], (T.qx3[:, 0:H].bitcast(dt.uint8),) + R("qx3", 0, H)[1:], 2.3)
    dma("Y", "std", T.oc[:, 4 * H:4 * C], (T.qx3[:, H:C].bitcast(dt.uint8),) + R("qx3", H, C)[1:], 2.3)
    dma("S", "stw", T.y[:, 0:H], R("yt", 0, H), 2.3)
    dma("Y", "sty", T.y[:, H:C], R("yt", H, C), 2.3)
    for k in range(4):
        dma("S", "sts", T.osc[4 * k:4 * k + 4, :], (T.sx3[32 * k:32 * k + 4, :],) + R("sx3")[1:], 2.0, 64)

    cnt = {"V": 0, "S": 0, "P": 0, "G": 0}
    known = {q: {} for q in Q}
    clock, seen, owed = {}, {}, {}

    def need(q, sem, n):
        if known[q].get(sem, 0) >= n:
            return
        Q[q].wait_ge(T.sem[sem], n)
        known[q][sem] = n
        for s, k in clock.get((sem, n), {}).items():
            known[q][s] = max(known[q].get(s, 0), k)

    for q, outs, ins, busy, done, kind, f, sem, n, lead in deal(calls):
        if kind == "land":
            owed[sem] = n
            enter(seen, outs, [], (sem, n))
            continue
        want = {}
        for s, k in clash(seen, outs, ins):
            want[s] = max(want.get(s, 0), k)
        for s in sorted(want, key=lambda s: s == q):
            need(q, s, want[s])
        if kind == "send":
            f()
            continue
        if kind == "run":
            cnt[q] += 1
            sem, n = q, cnt[q]
        f().then_inc(T.sem[sem], 16 if kind == "dma" else 1)
        clock[(sem, n)] = dict(known[q])
        owed[sem] = n
        enter(seen, outs, ins, (sem, n))
    g.wait_ge(T.sem.snd, sent[0])
    for s, n in owed.items():
        need("Y", s, n)
